import numpy as np
import ml_dtypes


def mxq(x, axis, fmt="e4m3"):
    dtype, down = {"e4m3": (ml_dtypes.float8_e4m3fn, 7), "e5m2": (ml_dtypes.float8_e5m2, 14)}[fmt]
    v = np.moveaxis(np.asarray(x, np.float32).astype(ml_dtypes.bfloat16).astype(np.float64), axis, -1)
    blocks = v.reshape(v.shape[:-1] + (-1, 32))
    amax = np.abs(blocks).max(-1, keepdims=True)
    byte = np.maximum(np.where(amax > 0, np.frexp(amax)[1] - 1 + 127, 0) - down, 1)
    scale = np.exp2(byte - 127.0)
    codes = (blocks / scale).astype(np.float32).astype(dtype).astype(np.float64)
    return np.moveaxis((codes * scale).reshape(v.shape), -1, axis)


WIDE = False


def mx_kscale(k):
    if not WIDE:
        return np.ones(k)
    levels = np.array([10, -10, 5, -5, 0])
    if k % 512:
        return np.exp2(np.random.permutation(np.resize(levels, k // 32))).repeat(32)
    a = np.empty((k // 512, 16))
    for p in range(k // 512):
        a[p, :8] = np.random.permutation(np.resize(levels, 8))
        for g in range(8):
            far = levels[np.abs(levels - a[p, g]) >= 10]
            a[p, g + 8] = far[np.random.randint(len(far))]
    return np.exp2(a.ravel()).repeat(32)


def f64(x):
    return np.asarray(x).astype(np.float64)


def striped(idx):
    return np.tile(idx.reshape(-1, 16).T, (8, 1)).astype(np.uint16)


def unstriped(offs):
    return offs[:16].T.reshape(-1).astype(np.int64)


def striped8(idx):
    return np.concatenate([x.reshape(-1, 16).T for x in idx]).astype(np.uint16)


def runs(offs, k):
    lists = np.stack([offs[16 * r : 16 * r + 16].T.reshape(-1) for r in range(8)]).astype(np.int64)
    return lists[np.arange(k) % 512 // 64]


def pack_weight(w):
    k, n = w.shape
    w = f64(np.asarray(w, np.float32).astype(ml_dtypes.bfloat16)).reshape(k // 32, 32, n)
    amax = np.abs(w).max(1)
    byte = np.clip(np.where(amax > 0, np.frexp(amax)[1] - 1 + 127 - 7, 1), 1, 254)
    scaled = (w * np.exp2(127.0 - byte)[:, None, :]).reshape(k, n).astype(np.float32)
    words = np.ascontiguousarray(scaled.reshape(k // 512, 128, 4, n).transpose(0, 1, 3, 2)).astype(ml_dtypes.float8_e4m3fn).view(np.uint8)
    return words, np.ascontiguousarray(byte.astype(np.uint8).reshape(k // 512, 16, n))


def unpack_weight(words, scales):
    g, p, n, _ = words.shape
    vals = np.ascontiguousarray(words).view(ml_dtypes.float8_e4m3fn).astype(np.float64) * np.repeat(np.exp2(scales.astype(np.float64) - 127.0), 8, axis=1)[..., None]
    return vals.transpose(0, 1, 3, 2).reshape(g * 512, n)


K, T, S, N, U = 512, 2048, 512, 512, 1024


def setup_inputs():
    n = np.random.standard_normal
    s = mx_kscale(K)[:, None]
    packed_xT = pack_weight(n((K, T)) * s)
    return {
        "x_words": packed_xT[0],
        "x_scales": packed_xT[1],
        "w1": (n((K, N)) / np.sqrt(K) / s).astype(np.float32),
        "par": n((N, U)).astype(np.float32),
        "m1": n((N, U)).astype(np.float32),
        "m2": np.random.uniform(0.5, 2.0, (N, U)).astype(np.float32),
        "offs": striped(np.random.permutation(T)[:S]),
        "ent": striped8(np.stack([np.random.permutation(U)[:S] for _ in range(8)])),
    }


def reference(x_words, x_scales, w1, par, m1, m2, offs, ent):
    xq = unpack_weight(x_words, x_scales)[:, unstriped(offs)]
    y = mxq(f64(w1), 0, "e4m3").T @ xq
    a = 0.75 * (f64(m1)[np.arange(N)[:, None], runs(ent, N)]) + 0.25 * y
    b = 0.875 * (f64(m2)[np.arange(N)[:, None], runs(ent, N)]) + 0.125 * ((y) ** 2)
    o = f64(par)[np.arange(N)[:, None], runs(ent, N)] - (0.5 * (a / np.sqrt(b)))
    out = f64(par).copy()
    out[np.arange(N)[:, None], runs(ent, N)] = o
    return out

@@ -1,0 +1,133 @@
+import math
+from contextlib import ExitStack
+
+import concourse.mybir as mybir
+from concourse.masks import make_identity
+
+K, T, S, N, U = 512, 2048, 512, 512, 1024
+FLOPS = 2 * K * N * S
+
+F32 = mybir.dt.float32
+BF16 = mybir.dt.bfloat16
+I32 = mybir.dt.int32
+U32 = mybir.dt.uint32
+U16 = mybir.dt.uint16
+U8 = mybir.dt.uint8
+FP8X4 = mybir.dt.float8_e4m3fn_x4
+ACT = mybir.ActivationFunctionType
+ALU = mybir.AluOpType
+
+P = 128
+PACK = 4
+TILES = N // P
+BLOCKS = S // P
+
+
+def tile_picked_sadam_none_p_kernel(tc, x_words, x_scales, w1, par, m1, m2, offs, ent, out):
+    nc = tc.nc
+    with ExitStack() as ctx:
+        lists = ctx.enter_context(tc.tile_pool(name="lists", bufs=1))
+        keep = ctx.enter_context(tc.tile_pool(name="keep", bufs=1))
+        psum = ctx.enter_context(tc.psum_pool(name="psum", bufs=2))
+
+        offs_sb = lists.tile([P, S // 16], U16, name="offs_sb")
+        ent_sb = lists.tile([P, S // 16], U16, name="ent_sb")
+
+        def rows(table, t):
+            return table.rearrange("(p t) u -> t p u", t=TILES)[t]
+
+        scale_table = keep.tile([P, T], U8, name="scale_table", align_bytes=64)
+        nc.vector.memset(scale_table[:].bitcast(I32), 0)
+        nine = keep.tile([P, 1], F32, name="nine")
+        nc.vector.memset(nine[:], 9.0)
+        third = keep.tile([P, 1], F32, name="third")
+        nc.scalar.activation(third[:], nine[:], ACT.Abs_reciprocal_sqrt)
+
+        nc.sync.dma_start(offs_sb[:], offs)
+        word_table = keep.tile([P, T], I32, name="word_table", align_bytes=64)
+        nc.sync.dma_start(word_table[:], x_words[0].rearrange("p c r -> p (c r)").bitcast(I32))
+        for q in range(4):
+            nc.scalar.dma_start(
+                scale_table[32 * q : 32 * q + 4, :].bitcast(I32),
+                x_scales[0, 4 * q : 4 * q + 4, :].bitcast(I32),
+            )
+        w_raw = keep.tile([P, PACK, N], F32, name="w_raw")
+        nc.sync.dma_start(w_raw[:], w1.rearrange("(p j) n -> p j n", j=PACK))
+        nc.sync.dma_start(ent_sb[:], ent)
+
+        m1_sb = [keep.tile([P, U], F32, name="m1_sb%d" % t) for t in range(TILES)]
+        m2_sb = [keep.tile([P, U], F32, name="m2_sb%d" % t) for t in range(TILES)]
+        par_sb = [keep.tile([P, U], F32, name="par_sb%d" % t) for t in range(TILES)]
+        for t in range(TILES):
+            nc.sync.dma_start(m2_sb[t][:], rows(m2, t))
+            nc.sync.dma_start(m1_sb[t][:], rows(m1, t))
+        for t in range(TILES):
+            nc.sync.dma_start(par_sb[t][:], rows(par, t))
+
+        ident = keep.tile([P, P], F32, name="ident")
+        make_identity(nc, ident[:])
+
+        x_codes = keep.tile([P, S], U32, name="x_codes", align_bytes=64)
+        x_plane = keep.tile([P, S], U8, name="x_plane", align_bytes=64)
+        nc.vector.tensor_copy(x_codes[:], word_table[:].bitcast(U32).indirect(offs_sb[:]))
+        nc.vector.tensor_copy(x_plane[:], scale_table[:].indirect(offs_sb[:]))
+
+        w_grouped = keep.tile([P, N * PACK], BF16, name="w_grouped", align_bytes=64)
+        nc.scalar.copy(
+            w_grouped[:].rearrange("p (t m j) -> p m t j", t=TILES, j=PACK),
+            w_raw[:].rearrange("p j (m t) -> p m t j", t=TILES),
+        )
+        w_codes = keep.tile([P, N], U32, name="w_codes", align_bytes=64)
+        w_plane = keep.tile([P, N], U8, name="w_plane", align_bytes=64)
+        nc.vector.quantize_mx(out=w_codes[:].bitcast(FP8X4), scales=w_plane[:], in_=w_grouped[:])
+
+        def turned_sum(bank, first, second):
+            for c in range(BLOCKS):
+                cols = slice(c * P, (c + 1) * P)
+                nc.tensor.matmul(bank[:, cols], first[:, cols], ident[:], start=True, stop=False, is_transpose=True)
+                nc.tensor.matmul(bank[:, cols], second[:, cols], ident[:], start=False, stop=True, is_transpose=True)
+
+        steps = []
+        for t in range(TILES):
+            cols = slice(t * P, (t + 1) * P)
+            y = psum.tile([P, S], F32, name="y")
+            nc.tensor.matmul_mx(
+                out=y[:],
+                lhsT=w_codes[:, cols].bitcast(FP8X4),
+                lhsT_scale=w_plane[:, cols],
+                rhs=x_codes[:].bitcast(FP8X4),
+                rhs_scale=x_plane[:],
+                start=True,
+                stop=True,
+            )
+            y_square = keep.tile([P, S], F32, name="y_square%d" % t)
+            nc.scalar.activation(y_square[:], y[:], ACT.Square, scale=1.0 / math.sqrt(7.0))
+            y_third = keep.tile([P, S], F32, name="y_third%d" % t)
+            nc.scalar.activation(y_third[:], y[:], ACT.Copy, scale=third[:])
+
+            m2_picked = keep.tile([P, S], F32, name="m2_picked%d" % t)
+            nc.vector.tensor_copy(m2_picked[:], m2_sb[t][:].indirect(ent_sb[:]))
+            m1_picked = keep.tile([P, S], F32, name="m1_picked%d" % t)
+            nc.vector.tensor_copy(m1_picked[:], m1_sb[t][:].indirect(ent_sb[:]))
+
+            b_turned = psum.tile([P, S], F32, name="b_turned")
+            turned_sum(b_turned, m2_picked, y_square)
+            r_turned = keep.tile([P, S], F32, name="r_turned%d" % t, tag="slot%d" % t)
+            nc.scalar.activation(r_turned[:], b_turned[:], ACT.Abs_reciprocal_sqrt, scale=0.875 / 0.375**2)
+            a_turned = psum.tile([P, S], F32, name="a_turned")
+            turned_sum(a_turned, m1_picked, y_third)
+            d_turned = keep.tile([P, S], F32, name="d_turned%d" % t)
+            nc.vector.tensor_tensor(d_turned[:], a_turned[:], r_turned[:], ALU.mult)
+            d_bank = psum.tile([P, S], F32, name="d_bank")
+            for c in range(BLOCKS):
+                blk = slice(c * P, (c + 1) * P)
+                nc.tensor.transpose(d_bank[:, blk], d_turned[:, blk], ident[:])
+            step = keep.tile([P, S], F32, name="step%d" % t)
+            nc.scalar.activation(step[:], d_bank[:], ACT.Copy, scale=-1.0)
+            steps.append(step)
+
+        for t in range(TILES):
+            par_picked = keep.tile([P, S], F32, name="par_picked%d" % t, tag="slot%d" % ((t + 1) % TILES))
+            nc.vector.tensor_copy(par_picked[:], par_sb[t][:].indirect(ent_sb[:]))
+            nc.vector.tensor_tensor(par_sb[t][:].indirect(ent_sb[:]), par_picked[:], steps[t][:], ALU.add)
+            nc.sync.dma_start(rows(out, t), par_sb[t][:])

@@ -87,8 +87,7 @@ def tile_picked_sadam_none_p_kernel(tc, x_words, x_scales, w1, par, m1, m2, offs
                 nc.tensor.matmul(bank[:, cols], first[:, cols], ident[:], start=True, stop=False, is_transpose=True)
                 nc.tensor.matmul(bank[:, cols], second[:, cols], ident[:], start=False, stop=True, is_transpose=True)
 
-        steps = []
-        for t in range(TILES):
+        def moments(t):
             cols = slice(t * P, (t + 1) * P)
             y = psum.tile([P, S], F32, name="y")
             nc.tensor.matmul_mx(
@@ -112,22 +111,28 @@ def tile_picked_sadam_none_p_kernel(tc, x_words, x_scales, w1, par, m1, m2, offs
 
             b_turned = psum.tile([P, S], F32, name="b_turned")
             turned_sum(b_turned, m2_picked, y_square)
-            r_turned = keep.tile([P, S], F32, name="r_turned%d" % t, tag="slot%d" % t)
+            r_turned = keep.tile([P, S], F32, name="r_turned%d" % t)
             nc.scalar.activation(r_turned[:], b_turned[:], ACT.Abs_reciprocal_sqrt, scale=0.875 / 0.375**2)
             a_turned = psum.tile([P, S], F32, name="a_turned")
             turned_sum(a_turned, m1_picked, y_third)
             d_turned = keep.tile([P, S], F32, name="d_turned%d" % t)
-            nc.vector.tensor_tensor(d_turned[:], a_turned[:], r_turned[:], ALU.mult)
+            a_copy = keep.tile([P, S], F32, name="a_copy%d" % t)
+            nc.scalar.copy(a_copy[:], a_turned[:])
+            nc.gpsimd.tensor_tensor(d_turned[:], a_copy[:], r_turned[:], ALU.mult)
+            return d_turned
+
+        def update(t, d_turned):
             d_bank = psum.tile([P, S], F32, name="d_bank")
             for c in range(BLOCKS):
                 blk = slice(c * P, (c + 1) * P)
                 nc.tensor.transpose(d_bank[:, blk], d_turned[:, blk], ident[:])
             step = keep.tile([P, S], F32, name="step%d" % t)
             nc.scalar.activation(step[:], d_bank[:], ACT.Copy, scale=-1.0)
-            steps.append(step)
-
-        for t in range(TILES):
-            par_picked = keep.tile([P, S], F32, name="par_picked%d" % t, tag="slot%d" % ((t + 1) % TILES))
+            par_picked = keep.tile([P, S], F32, name="par_picked%d" % t)
             nc.vector.tensor_copy(par_picked[:], par_sb[t][:].indirect(ent_sb[:]))
-            nc.vector.tensor_tensor(par_sb[t][:].indirect(ent_sb[:]), par_picked[:], steps[t][:], ALU.add)
+            nc.vector.tensor_tensor(par_sb[t][:].indirect(ent_sb[:]), par_picked[:], step[:], ALU.add)
             nc.sync.dma_start(rows(out, t), par_sb[t][:])
+
+        turned = [moments(t) for t in range(TILES)]
+        for t in range(TILES):
+            update(t, turned[t])

@@ -73,10 +73,10 @@ def tile_picked_sadam_none_p_kernel(tc, x_words, x_scales, w1, par, m1, m2, offs
         nc.vector.tensor_copy(x_plane[:], scale_table[:].indirect(offs_sb[:]))
 
         w_grouped = keep.tile([P, N * PACK], BF16, name="w_grouped", align_bytes=64)
-        nc.scalar.copy(
-            w_grouped[:].rearrange("p (t m j) -> p m t j", t=TILES, j=PACK),
-            w_raw[:].rearrange("p j (m t) -> p m t j", t=TILES),
-        )
+        grouped_view = w_grouped[:].rearrange("p (t m j) -> p m t j", t=TILES, j=PACK)
+        raw_view = w_raw[:].rearrange("p j (m t) -> p m t j", t=TILES)
+        nc.scalar.copy(grouped_view[:, :, :2, :], raw_view[:, :, :2, :])
+        nc.gpsimd.tensor_scalar(grouped_view[:, :, 2:, :], raw_view[:, :, 2:, :], 1.0, 0.0, ALU.mult, ALU.add)
         w_codes = keep.tile([P, N], U32, name="w_codes", align_bytes=64)
         w_plane = keep.tile([P, N], U8, name="w_plane", align_bytes=64)
         nc.vector.quantize_mx(out=w_codes[:].bitcast(FP8X4), scales=w_plane[:], in_=w_grouped[:])

@@ -28,7 +28,7 @@ def tile_picked_sadam_none_p_kernel(tc, x_words, x_scales, w1, par, m1, m2, offs
     with ExitStack() as ctx:
         lists = ctx.enter_context(tc.tile_pool(name="lists", bufs=1))
         keep = ctx.enter_context(tc.tile_pool(name="keep", bufs=1))
-        psum = ctx.enter_context(tc.psum_pool(name="psum", bufs=2))
+        psum = ctx.enter_context(tc.psum_pool(name="psum", bufs=1))
 
         offs_sb = lists.tile([P, S // 16], U16, name="offs_sb")
         ent_sb = lists.tile([P, S // 16], U16, name="ent_sb")
@@ -81,15 +81,25 @@ def tile_picked_sadam_none_p_kernel(tc, x_words, x_scales, w1, par, m1, m2, offs
         w_plane = keep.tile([P, N], U8, name="w_plane", align_bytes=64)
         nc.vector.quantize_mx(out=w_codes[:].bitcast(FP8X4), scales=w_plane[:], in_=w_grouped[:])
 
-        def turned_sum(bank, first, second):
+        def bank(number):
+            return psum.tile([P, S], F32, name="bank%d" % number)
+
+        def turn(target, source, start, stop):
             for c in range(BLOCKS):
                 cols = slice(c * P, (c + 1) * P)
-                nc.tensor.matmul(bank[:, cols], first[:, cols], ident[:], start=True, stop=False, is_transpose=True)
-                nc.tensor.matmul(bank[:, cols], second[:, cols], ident[:], start=False, stop=True, is_transpose=True)
+                nc.tensor.matmul(
+                    target[:, cols],
+                    source[:, cols],
+                    ident[:],
+                    start=start and c == 0,
+                    stop=stop and c == BLOCKS - 1,
+                    is_transpose=True,
+                )
 
-        def moments(t):
+        ys = []
+        for t in range(TILES):
             cols = slice(t * P, (t + 1) * P)
-            y = psum.tile([P, S], F32, name="y")
+            y = bank(t)
             nc.tensor.matmul_mx(
                 out=y[:],
                 lhsT=w_codes[:, cols].bitcast(FP8X4),
@@ -99,22 +109,27 @@ def tile_picked_sadam_none_p_kernel(tc, x_words, x_scales, w1, par, m1, m2, offs
                 start=True,
                 stop=True,
             )
+            ys.append(y)
+
+        def moments(t):
             y_square = keep.tile([P, S], F32, name="y_square%d" % t)
-            nc.scalar.activation(y_square[:], y[:], ACT.Square, scale=1.0 / math.sqrt(7.0))
+            nc.scalar.activation(y_square[:], ys[t][:], ACT.Square, scale=1.0 / math.sqrt(7.0))
             y_third = keep.tile([P, S], F32, name="y_third%d" % t)
-            nc.scalar.activation(y_third[:], y[:], ACT.Copy, scale=third[:])
+            nc.scalar.activation(y_third[:], ys[t][:], ACT.Copy, scale=third[:])
+            b_turned = bank((TILES + 2 * t) % 8)
+            a_turned = bank((TILES + 2 * t + 1) % 8)
+            turn(b_turned, y_square, True, False)
+            turn(a_turned, y_third, True, False)
 
             m2_picked = keep.tile([P, S], F32, name="m2_picked%d" % t)
             nc.vector.tensor_copy(m2_picked[:], m2_sb[t][:].indirect(ent_sb[:]))
             m1_picked = keep.tile([P, S], F32, name="m1_picked%d" % t)
             nc.vector.tensor_copy(m1_picked[:], m1_sb[t][:].indirect(ent_sb[:]))
 
-            b_turned = psum.tile([P, S], F32, name="b_turned")
-            turned_sum(b_turned, m2_picked, y_square)
+            turn(b_turned, m2_picked, False, True)
             r_turned = keep.tile([P, S], F32, name="r_turned%d" % t)
             nc.scalar.activation(r_turned[:], b_turned[:], ACT.Abs_reciprocal_sqrt, scale=0.875 / 0.375**2)
-            a_turned = psum.tile([P, S], F32, name="a_turned")
-            turned_sum(a_turned, m1_picked, y_third)
+            turn(a_turned, m1_picked, False, True)
             d_turned = keep.tile([P, S], F32, name="d_turned%d" % t)
             a_copy = keep.tile([P, S], F32, name="a_copy%d" % t)
             nc.scalar.copy(a_copy[:], a_turned[:])
@@ -122,10 +137,8 @@ def tile_picked_sadam_none_p_kernel(tc, x_words, x_scales, w1, par, m1, m2, offs
             return d_turned
 
         def update(t, d_turned):
-            d_bank = psum.tile([P, S], F32, name="d_bank")
-            for c in range(BLOCKS):
-                blk = slice(c * P, (c + 1) * P)
-                nc.tensor.transpose(d_bank[:, blk], d_turned[:, blk], ident[:])
+            d_bank = bank(TILES - 1)
+            turn(d_bank, d_turned, True, True)
             step = keep.tile([P, S], F32, name="step%d" % t)
             nc.scalar.activation(step[:], d_bank[:], ACT.Copy, scale=-1.0)
             par_picked = keep.tile([P, S], F32, name="par_picked%d" % t)

@@ -21,6 +21,7 @@ P = 128
 PACK = 4
 TILES = N // P
 BLOCKS = S // P
+VECTOR_SHARE = 80
 
 
 def tile_picked_sadam_none_p_kernel(tc, x_words, x_scales, w1, par, m1, m2, offs, ent, out):
@@ -37,22 +38,21 @@ def tile_picked_sadam_none_p_kernel(tc, x_words, x_scales, w1, par, m1, m2, offs
             return table.rearrange("(p t) u -> t p u", t=TILES)[t]
 
         scale_table = keep.tile([P, T], U8, name="scale_table", align_bytes=64)
-        nc.vector.memset(scale_table[:].bitcast(I32), 0)
+        for first, end in ((0, 16), (32, 64), (64, P)):
+            nc.gpsimd.memset(scale_table[first:end, :].bitcast(I32), 0)
+        x_plane = keep.tile([P, S], U8, name="x_plane", align_bytes=64)
+        nc.gpsimd.memset(x_plane[:].bitcast(I32), 0)
         nine = keep.tile([P, 1], F32, name="nine")
         nc.vector.memset(nine[:], 9.0)
         third = keep.tile([P, 1], F32, name="third")
         nc.scalar.activation(third[:], nine[:], ACT.Abs_reciprocal_sqrt)
 
         nc.sync.dma_start(offs_sb[:], offs)
-        word_table = keep.tile([P, T], I32, name="word_table", align_bytes=64)
-        nc.sync.dma_start(word_table[:], x_words[0].rearrange("p c r -> p (c r)").bitcast(I32))
-        for q in range(4):
-            nc.scalar.dma_start(
-                scale_table[32 * q : 32 * q + 4, :].bitcast(I32),
-                x_scales[0, 4 * q : 4 * q + 4, :].bitcast(I32),
-            )
+        nc.sync.dma_start(scale_table[16:32, :].bitcast(I32), x_scales[0].bitcast(I32))
         w_raw = keep.tile([P, PACK, N], F32, name="w_raw")
         nc.sync.dma_start(w_raw[:], w1.rearrange("(p j) n -> p j n", j=PACK))
+        word_table = keep.tile([P, T], I32, name="word_table", align_bytes=64)
+        nc.sync.dma_start(word_table[:], x_words[0].rearrange("p c r -> p (c r)").bitcast(I32))
         nc.sync.dma_start(ent_sb[:], ent)
 
         m1_sb = [keep.tile([P, U], F32, name="m1_sb%d" % t) for t in range(TILES)]
@@ -68,15 +68,20 @@ def tile_picked_sadam_none_p_kernel(tc, x_words, x_scales, w1, par, m1, m2, offs
         make_identity(nc, ident[:])
 
         x_codes = keep.tile([P, S], U32, name="x_codes", align_bytes=64)
-        x_plane = keep.tile([P, S], U8, name="x_plane", align_bytes=64)
+        scale_picked = keep.tile([P, S], U8, name="scale_picked", align_bytes=64)
+        nc.vector.tensor_copy(scale_picked[:], scale_table[:].indirect(offs_sb[:]))
+        for q in range(4):
+            nc.scalar.dma_start(
+                x_plane[32 * q : 32 * q + 4, :].bitcast(I32),
+                scale_picked[16 + 4 * q : 20 + 4 * q, :].bitcast(I32),
+            )
         nc.vector.tensor_copy(x_codes[:], word_table[:].bitcast(U32).indirect(offs_sb[:]))
-        nc.vector.tensor_copy(x_plane[:], scale_table[:].indirect(offs_sb[:]))
 
         w_grouped = keep.tile([P, N * PACK], BF16, name="w_grouped", align_bytes=64)
         grouped_view = w_grouped[:].rearrange("p (t m j) -> p m t j", t=TILES, j=PACK)
         raw_view = w_raw[:].rearrange("p j (m t) -> p m t j", t=TILES)
-        nc.scalar.copy(grouped_view[:, :, :2, :], raw_view[:, :, :2, :])
-        nc.gpsimd.tensor_scalar(grouped_view[:, :, 2:, :], raw_view[:, :, 2:, :], 1.0, 0.0, ALU.mult, ALU.add)
+        nc.vector.tensor_copy(grouped_view[:, :VECTOR_SHARE], raw_view[:, :VECTOR_SHARE])
+        nc.scalar.copy(grouped_view[:, VECTOR_SHARE:], raw_view[:, VECTOR_SHARE:])
         w_codes = keep.tile([P, N], U32, name="w_codes", align_bytes=64)
         w_plane = keep.tile([P, N], U8, name="w_plane", align_bytes=64)
         nc.vector.quantize_mx(out=w_codes[:].bitcast(FP8X4), scales=w_plane[:], in_=w_grouped[:])

@@ -61,8 +61,11 @@ def tile_picked_sadam_none_p_kernel(tc, x_words, x_scales, w1, par, m1, m2, offs
         for t in range(TILES):
             nc.sync.dma_start(m2_sb[t][:], rows(m2, t))
             nc.sync.dma_start(m1_sb[t][:], rows(m1, t))
+        held = TILES - 2
+        par_held = keep.tile([P, U], F32, name="par_held")
+        windows = [par_held if t == held else par_sb[t] for t in range(TILES)]
         for t in range(TILES):
-            nc.sync.dma_start(par_sb[t][:], rows(par, t))
+            nc.sync.dma_start(windows[t][:], rows(par, t))
 
         ident = keep.tile([P, P], F32, name="ident")
         make_identity(nc, ident[:])
@@ -141,16 +144,16 @@ def tile_picked_sadam_none_p_kernel(tc, x_words, x_scales, w1, par, m1, m2, offs
             nc.gpsimd.tensor_tensor(d_turned[:], a_copy[:], r_turned[:], ALU.mult)
             return d_turned
 
-        def update(t, d_turned):
-            d_bank = bank(TILES - 1)
-            turn(d_bank, d_turned, True, True)
-            step = keep.tile([P, S], F32, name="step%d" % t)
-            nc.scalar.activation(step[:], d_bank[:], ACT.Copy, scale=-1.0)
-            par_picked = keep.tile([P, S], F32, name="par_picked%d" % t)
-            nc.vector.tensor_copy(par_picked[:], par_sb[t][:].indirect(ent_sb[:]))
-            nc.vector.tensor_tensor(par_sb[t][:].indirect(ent_sb[:]), par_picked[:], step[:], ALU.add)
-            nc.sync.dma_start(rows(out, t), par_sb[t][:])
-
         turned = [moments(t) for t in range(TILES)]
+        par_picked = [keep.tile([P, S], F32, name="par_picked%d" % t) for t in range(TILES)]
         for t in range(TILES):
-            update(t, turned[t])
+            nc.vector.tensor_copy(par_picked[t][:], windows[t][:].indirect(ent_sb[:]))
+        nc.scalar.copy(par_sb[held][:], par_held[:])
+
+        step = keep.tile([P, TILES, S], F32, name="par_held")
+        for t, number in enumerate((3, 2, 3, 2)):
+            d_bank = bank(number)
+            turn(d_bank, turned[t], True, True)
+            nc.scalar.activation(step[:, t, :], d_bank[:], ACT.Copy, scale=-1.0)
+            nc.vector.tensor_tensor(par_sb[t][:].indirect(ent_sb[:]), par_picked[t][:], step[:, t, :], ALU.add)
+            nc.sync.dma_start(rows(out, t), par_sb[t][:])

@@ -19,9 +19,15 @@ ALU = mybir.AluOpType
 
 P = 128
 PACK = 4
+GROUP = 16
+QUADRANT = 32
+BANKS = 8
 TILES = N // P
 BLOCKS = S // P
-VECTOR_SHARE = 80
+SCALE_ROWS = K // 32
+ROWS_PER_QUADRANT = SCALE_ROWS * QUADRANT // P
+SCALE_FIRST = QUADRANT - SCALE_ROWS
+VECTOR_SHARE = 96
 
 
 def tile_picked_sadam_none_p_kernel(tc, x_words, x_scales, w1, par, m1, m2, offs, ent, out):
@@ -31,14 +37,14 @@ def tile_picked_sadam_none_p_kernel(tc, x_words, x_scales, w1, par, m1, m2, offs
         keep = ctx.enter_context(tc.tile_pool(name="keep", bufs=1))
         psum = ctx.enter_context(tc.psum_pool(name="psum", bufs=1))
 
-        offs_sb = lists.tile([P, S // 16], U16, name="offs_sb")
-        ent_sb = lists.tile([P, S // 16], U16, name="ent_sb")
+        offs_sb = lists.tile([P, S // GROUP], U16, name="offs_sb")
+        ent_sb = lists.tile([P, S // GROUP], U16, name="ent_sb")
 
         def rows(table, t):
             return table.rearrange("(p t) u -> t p u", t=TILES)[t]
 
         scale_table = keep.tile([P, T], U8, name="scale_table", align_bytes=64)
-        for first, end in ((0, 16), (32, 64), (64, P)):
+        for first, end in ((0, SCALE_FIRST), (QUADRANT, P // 2), (P // 2, P)):
             nc.gpsimd.memset(scale_table[first:end, :].bitcast(I32), 0)
         x_plane = keep.tile([P, S], U8, name="x_plane", align_bytes=64)
         nc.gpsimd.memset(x_plane[:].bitcast(I32), 0)
@@ -48,7 +54,7 @@ def tile_picked_sadam_none_p_kernel(tc, x_words, x_scales, w1, par, m1, m2, offs
         nc.scalar.activation(third[:], nine[:], ACT.Abs_reciprocal_sqrt)
 
         nc.sync.dma_start(offs_sb[:], offs)
-        nc.sync.dma_start(scale_table[16:32, :].bitcast(I32), x_scales[0].bitcast(I32))
+        nc.sync.dma_start(scale_table[SCALE_FIRST:QUADRANT, :].bitcast(I32), x_scales[0].bitcast(I32))
         w_raw = keep.tile([P, PACK, N], F32, name="w_raw")
         nc.sync.dma_start(w_raw[:], w1.rearrange("(p j) n -> p j n", j=PACK))
         word_table = keep.tile([P, T], I32, name="word_table", align_bytes=64)
@@ -57,15 +63,15 @@ def tile_picked_sadam_none_p_kernel(tc, x_words, x_scales, w1, par, m1, m2, offs
 
         m1_sb = [keep.tile([P, U], F32, name="m1_sb%d" % t) for t in range(TILES)]
         m2_sb = [keep.tile([P, U], F32, name="m2_sb%d" % t) for t in range(TILES)]
-        par_sb = [keep.tile([P, U], F32, name="par_sb%d" % t) for t in range(TILES)]
+        scatter_windows = [keep.tile([P, U], F32, name="par_sb%d" % t) for t in range(TILES)]
         for t in range(TILES):
             nc.sync.dma_start(m2_sb[t][:], rows(m2, t))
             nc.sync.dma_start(m1_sb[t][:], rows(m1, t))
         held = TILES - 2
         par_held = keep.tile([P, U], F32, name="par_held")
-        windows = [par_held if t == held else par_sb[t] for t in range(TILES)]
+        gather_windows = [par_held if t == held else scatter_windows[t] for t in range(TILES)]
         for t in range(TILES):
-            nc.sync.dma_start(windows[t][:], rows(par, t))
+            nc.sync.dma_start(gather_windows[t][:], rows(par, t))
 
         ident = keep.tile([P, P], F32, name="ident")
         make_identity(nc, ident[:])
@@ -73,10 +79,12 @@ def tile_picked_sadam_none_p_kernel(tc, x_words, x_scales, w1, par, m1, m2, offs
         x_codes = keep.tile([P, S], U32, name="x_codes", align_bytes=64)
         scale_picked = keep.tile([P, S], U8, name="scale_picked", align_bytes=64)
         nc.vector.tensor_copy(scale_picked[:], scale_table[:].indirect(offs_sb[:]))
-        for q in range(4):
+        for quadrant in range(P // QUADRANT):
+            source = SCALE_FIRST + ROWS_PER_QUADRANT * quadrant
+            target = QUADRANT * quadrant
             nc.scalar.dma_start(
-                x_plane[32 * q : 32 * q + 4, :].bitcast(I32),
-                scale_picked[16 + 4 * q : 20 + 4 * q, :].bitcast(I32),
+                x_plane[target : target + ROWS_PER_QUADRANT, :].bitcast(I32),
+                scale_picked[source : source + ROWS_PER_QUADRANT, :].bitcast(I32),
             )
         nc.vector.tensor_copy(x_codes[:], word_table[:].bitcast(U32).indirect(offs_sb[:]))
 
@@ -91,6 +99,9 @@ def tile_picked_sadam_none_p_kernel(tc, x_words, x_scales, w1, par, m1, m2, offs
 
         def bank(number):
             return psum.tile([P, S], F32, name="bank%d" % number)
+
+        def sum_banks(t):
+            return (TILES + 2 * t) % BANKS, (TILES + 2 * t + 1) % BANKS
 
         def turn(target, source, start, stop):
             for c in range(BLOCKS):
@@ -119,13 +130,14 @@ def tile_picked_sadam_none_p_kernel(tc, x_words, x_scales, w1, par, m1, m2, offs
             )
             ys.append(y)
 
-        def moments(t):
+        def turned_step(t):
             y_square = keep.tile([P, S], F32, name="y_square%d" % t)
             nc.scalar.activation(y_square[:], ys[t][:], ACT.Square, scale=1.0 / math.sqrt(7.0))
             y_third = keep.tile([P, S], F32, name="y_third%d" % t)
             nc.scalar.activation(y_third[:], ys[t][:], ACT.Copy, scale=third[:])
-            b_turned = bank((TILES + 2 * t) % 8)
-            a_turned = bank((TILES + 2 * t + 1) % 8)
+            b_number, a_number = sum_banks(t)
+            b_turned = bank(b_number)
+            a_turned = bank(a_number)
             turn(b_turned, y_square, True, False)
             turn(a_turned, y_third, True, False)
 
@@ -144,16 +156,19 @@ def tile_picked_sadam_none_p_kernel(tc, x_words, x_scales, w1, par, m1, m2, offs
             nc.gpsimd.tensor_tensor(d_turned[:], a_copy[:], r_turned[:], ALU.mult)
             return d_turned
 
-        turned = [moments(t) for t in range(TILES)]
+        turned = [turned_step(t) for t in range(TILES)]
         par_picked = [keep.tile([P, S], F32, name="par_picked%d" % t) for t in range(TILES)]
         for t in range(TILES):
-            nc.vector.tensor_copy(par_picked[t][:], windows[t][:].indirect(ent_sb[:]))
-        nc.scalar.copy(par_sb[held][:], par_held[:])
+            nc.vector.tensor_copy(par_picked[t][:], gather_windows[t][:].indirect(ent_sb[:]))
+        nc.scalar.copy(scatter_windows[held][:], par_held[:])
 
-        step = keep.tile([P, TILES, S], F32, name="par_held")
-        for t, number in enumerate((3, 2, 3, 2)):
-            d_bank = bank(number)
+        minus_step = keep.tile([P, TILES, S], F32, name="par_held")
+        b_last, a_last = sum_banks(TILES - 1)
+        for t in range(TILES):
+            d_bank = bank(a_last if t % 2 == 0 else b_last)
             turn(d_bank, turned[t], True, True)
-            nc.scalar.activation(step[:, t, :], d_bank[:], ACT.Copy, scale=-1.0)
-            nc.vector.tensor_tensor(par_sb[t][:].indirect(ent_sb[:]), par_picked[t][:], step[:, t, :], ALU.add)
-            nc.sync.dma_start(rows(out, t), par_sb[t][:])
+            nc.scalar.activation(minus_step[:, t, :], d_bank[:], ACT.Copy, scale=-1.0)
+            nc.vector.tensor_tensor(
+                scatter_windows[t][:].indirect(ent_sb[:]), par_picked[t][:], minus_step[:, t, :], ALU.add
+            )
+            nc.sync.dma_start(rows(out, t), scatter_windows[t][:])

@@ -64,14 +64,15 @@ def tile_picked_sadam_none_p_kernel(tc, x_words, x_scales, w1, par, m1, m2, offs
         m1_sb = [keep.tile([P, U], F32, name="m1_sb%d" % t) for t in range(TILES)]
         m2_sb = [keep.tile([P, U], F32, name="m2_sb%d" % t) for t in range(TILES)]
         scatter_windows = [keep.tile([P, U], F32, name="par_sb%d" % t) for t in range(TILES)]
-        for t in range(TILES):
-            nc.sync.dma_start(m2_sb[t][:], rows(m2, t))
-            nc.sync.dma_start(m1_sb[t][:], rows(m1, t))
         held = TILES - 2
         par_held = keep.tile([P, U], F32, name="par_held")
         gather_windows = [par_held if t == held else scatter_windows[t] for t in range(TILES)]
-        for t in range(TILES):
-            nc.sync.dma_start(gather_windows[t][:], rows(par, t))
+        for first in range(0, TILES, 2):
+            for t in (first, first + 1):
+                nc.sync.dma_start(m2_sb[t][:], rows(m2, t))
+                nc.sync.dma_start(m1_sb[t][:], rows(m1, t))
+            for t in (first, first + 1):
+                nc.sync.dma_start(gather_windows[t][:], rows(par, t))
 
         ident = keep.tile([P, P], F32, name="ident")
         make_identity(nc, ident[:])
@@ -156,19 +157,31 @@ def tile_picked_sadam_none_p_kernel(tc, x_words, x_scales, w1, par, m1, m2, offs
             nc.gpsimd.tensor_tensor(d_turned[:], a_copy[:], r_turned[:], ALU.mult)
             return d_turned
 
-        turned = [turned_step(t) for t in range(TILES)]
         par_picked = [keep.tile([P, S], F32, name="par_picked%d" % t) for t in range(TILES)]
-        for t in range(TILES):
-            nc.vector.tensor_copy(par_picked[t][:], gather_windows[t][:].indirect(ent_sb[:]))
-        nc.scalar.copy(scatter_windows[held][:], par_held[:])
 
-        minus_step = keep.tile([P, TILES, S], F32, name="par_held")
-        b_last, a_last = sum_banks(TILES - 1)
-        for t in range(TILES):
-            d_bank = bank(a_last if t % 2 == 0 else b_last)
-            turn(d_bank, turned[t], True, True)
-            nc.scalar.activation(minus_step[:, t, :], d_bank[:], ACT.Copy, scale=-1.0)
+        def gather_par(t):
+            nc.vector.tensor_copy(par_picked[t][:], gather_windows[t][:].indirect(ent_sb[:]))
+
+        def update(t, turned, slot):
+            d_bank = bank(sum_banks(t)[1])
+            turn(d_bank, turned, True, True)
+            minus_step = keep.tile([P, S], F32, name=slot)
+            nc.scalar.activation(minus_step[:], d_bank[:], ACT.Copy, scale=-1.0)
             nc.vector.tensor_tensor(
-                scatter_windows[t][:].indirect(ent_sb[:]), par_picked[t][:], minus_step[:, t, :], ALU.add
+                scatter_windows[t][:].indirect(ent_sb[:]), par_picked[t][:], minus_step[:], ALU.add
             )
             nc.sync.dma_start(rows(out, t), scatter_windows[t][:])
+
+        turned0 = turned_step(0)
+        turned1 = turned_step(1)
+        gather_par(0)
+        gather_par(1)
+        turned2 = turned_step(2)
+        update(0, turned0, "m2_sb2")
+        turned3 = turned_step(3)
+        update(1, turned1, "m2_sb3")
+        gather_par(2)
+        gather_par(3)
+        nc.scalar.copy(scatter_windows[held][:], par_held[:])
+        update(2, turned2, "par_held")
+        update(3, turned3, "step3")

@@ -67,12 +67,14 @@ def tile_picked_sadam_none_p_kernel(tc, x_words, x_scales, w1, par, m1, m2, offs
         held = TILES - 2
         par_held = keep.tile([P, U], F32, name="par_held")
         gather_windows = [par_held if t == held else scatter_windows[t] for t in range(TILES)]
-        for first in range(0, TILES, 2):
-            for t in (first, first + 1):
-                nc.sync.dma_start(m2_sb[t][:], rows(m2, t))
-                nc.sync.dma_start(m1_sb[t][:], rows(m1, t))
-            for t in (first, first + 1):
-                nc.sync.dma_start(gather_windows[t][:], rows(par, t))
+        tables = {"m2": (m2_sb, m2), "m1": (m1_sb, m1), "par": (gather_windows, par)}
+        for name, t in (
+            ("par", 0), ("m2", 1), ("m2", 0), ("m1", 0), ("m2", 2), ("m1", 1),
+            ("m1", 2), ("par", 1), ("m2", 3), ("m1", 3),
+            ("par", 2), ("par", 3),
+        ):
+            tiles, table = tables[name]
+            nc.sync.dma_start(tiles[t][:], rows(table, t))
 
         ident = keep.tile([P, P], F32, name="ident")
         make_identity(nc, ident[:])
@@ -101,9 +103,6 @@ def tile_picked_sadam_none_p_kernel(tc, x_words, x_scales, w1, par, m1, m2, offs
         def bank(number):
             return psum.tile([P, S], F32, name="bank%d" % number)
 
-        def sum_banks(t):
-            return (TILES + 2 * t) % BANKS, (TILES + 2 * t + 1) % BANKS
-
         def turn(target, source, start, stop):
             for c in range(BLOCKS):
                 cols = slice(c * P, (c + 1) * P)
@@ -116,10 +115,9 @@ def tile_picked_sadam_none_p_kernel(tc, x_words, x_scales, w1, par, m1, m2, offs
                     is_transpose=True,
                 )
 
-        ys = []
-        for t in range(TILES):
+        def project(t, number):
             cols = slice(t * P, (t + 1) * P)
-            y = bank(t)
+            y = bank(number)
             nc.tensor.matmul_mx(
                 out=y[:],
                 lhsT=w_codes[:, cols].bitcast(FP8X4),
@@ -129,59 +127,79 @@ def tile_picked_sadam_none_p_kernel(tc, x_words, x_scales, w1, par, m1, m2, offs
                 start=True,
                 stop=True,
             )
-            ys.append(y)
+            return y
 
-        def turned_step(t):
-            y_square = keep.tile([P, S], F32, name="y_square%d" % t)
-            nc.scalar.activation(y_square[:], ys[t][:], ACT.Square, scale=1.0 / math.sqrt(7.0))
-            y_third = keep.tile([P, S], F32, name="y_third%d" % t)
-            nc.scalar.activation(y_third[:], ys[t][:], ACT.Copy, scale=third[:])
-            b_number, a_number = sum_banks(t)
-            b_turned = bank(b_number)
-            a_turned = bank(a_number)
+        def gather(name, window, t):
+            picked = keep.tile([P, S], F32, name="%s_picked%d" % (name, t))
+            nc.vector.tensor_copy(picked[:], window[:].indirect(ent_sb[:]))
+            return picked
+
+        def turned_root(y, m2_picked, number, y_square, r_turned):
+            nc.scalar.activation(y_square, y[:], ACT.Square, scale=1.0 / math.sqrt(7.0))
+            b_turned = bank(number)
             turn(b_turned, y_square, True, False)
-            turn(a_turned, y_third, True, False)
-
-            m2_picked = keep.tile([P, S], F32, name="m2_picked%d" % t)
-            nc.vector.tensor_copy(m2_picked[:], m2_sb[t][:].indirect(ent_sb[:]))
-            m1_picked = keep.tile([P, S], F32, name="m1_picked%d" % t)
-            nc.vector.tensor_copy(m1_picked[:], m1_sb[t][:].indirect(ent_sb[:]))
-
             turn(b_turned, m2_picked, False, True)
-            r_turned = keep.tile([P, S], F32, name="r_turned%d" % t)
-            nc.scalar.activation(r_turned[:], b_turned[:], ACT.Abs_reciprocal_sqrt, scale=0.875 / 0.375**2)
+            nc.scalar.activation(r_turned, b_turned[:], ACT.Abs_reciprocal_sqrt, scale=0.875 / 0.375**2)
+            return r_turned
+
+        def third_of(y, y_third):
+            nc.scalar.activation(y_third, y[:], ACT.Copy, scale=third[:])
+            return y_third
+
+        def turned_step(t, y_third, m1_picked, r_turned, number):
+            a_turned = bank(number)
+            turn(a_turned, y_third, True, False)
             turn(a_turned, m1_picked, False, True)
             d_turned = keep.tile([P, S], F32, name="d_turned%d" % t)
             a_copy = keep.tile([P, S], F32, name="a_copy%d" % t)
             nc.scalar.copy(a_copy[:], a_turned[:])
-            nc.gpsimd.tensor_tensor(d_turned[:], a_copy[:], r_turned[:], ALU.mult)
+            nc.gpsimd.tensor_tensor(d_turned[:], a_copy[:], r_turned, ALU.mult)
             return d_turned
 
-        par_picked = [keep.tile([P, S], F32, name="par_picked%d" % t) for t in range(TILES)]
-
-        def gather_par(t):
-            nc.vector.tensor_copy(par_picked[t][:], gather_windows[t][:].indirect(ent_sb[:]))
-
-        def update(t, turned, slot):
-            d_bank = bank(sum_banks(t)[1])
+        def turned_back(turned, number):
+            d_bank = bank(number)
             turn(d_bank, turned, True, True)
+            return d_bank
+
+        def update(t, step, par_picked, slot):
             minus_step = keep.tile([P, S], F32, name=slot)
-            nc.scalar.activation(minus_step[:], d_bank[:], ACT.Copy, scale=-1.0)
+            nc.scalar.activation(minus_step[:], step[:], ACT.Copy, scale=-1.0)
             nc.vector.tensor_tensor(
-                scatter_windows[t][:].indirect(ent_sb[:]), par_picked[t][:], minus_step[:], ALU.add
+                scatter_windows[t][:].indirect(ent_sb[:]), par_picked[:], minus_step[:], ALU.add
             )
             nc.sync.dma_start(rows(out, t), scatter_windows[t][:])
 
-        turned0 = turned_step(0)
-        turned1 = turned_step(1)
-        gather_par(0)
-        gather_par(1)
-        turned2 = turned_step(2)
-        update(0, turned0, "m2_sb2")
-        turned3 = turned_step(3)
-        update(1, turned1, "m2_sb3")
-        gather_par(2)
-        gather_par(3)
+        ys = [project(t, t) for t in range(TILES)]
+        par0 = gather("par", gather_windows[0], 0)
+        m2_picked1 = gather("m2", m2_sb[1], 1)
+        terms0 = keep.tile([P, 2, S], F32, name="terms0")
+        nc.scalar.activation(terms0[:, 0, :], ys[0][:], ACT.Square, scale=1.0 / math.sqrt(7.0))
+        third_of(ys[0], terms0[:, 1, :])
+        b0 = keep.tile([P, S], F32, name="b0")
+        nc.vector.tensor_tensor(b0[:], m2_sb[0][:].indirect(ent_sb[:]), terms0[:, 0, :], ALU.add)
+        r0 = keep.tile([P, S], F32, name="r0")
+        nc.scalar.activation(r0[:], b0[:], ACT.Abs_reciprocal_sqrt, scale=0.875 / 0.375**2)
+        a0 = keep.tile([P, S], F32, name="a0")
+        nc.vector.tensor_tensor(a0[:], m1_sb[0][:].indirect(ent_sb[:]), terms0[:, 1, :], ALU.add)
+        step0 = keep.tile([P, S], F32, name="step0")
+        nc.gpsimd.tensor_tensor(step0[:], a0[:], r0[:], ALU.mult)
+        m2_picked2 = gather("m2", m2_sb[2], 2)
+        update(0, step0, par0, "m2_sb2")
+
+        terms1 = keep.tile([P, 2, S], F32, name="terms1")
+        late = keep.tile([P, 5, S], F32, name="step0")
+        roots = keep.tile([P, 2, S], F32, name="roots")
+        root1 = turned_root(ys[1], m2_picked1, 4, terms1[:, 0, :], late[:, 0, :])
+        turned1 = turned_step(1, third_of(ys[1], terms1[:, 1, :]), gather("m1", m1_sb[1], 1), root1, 5)
+        root2 = turned_root(ys[2], m2_picked2, 6, late[:, 1, :], roots[:, 0, :])
+        turned2 = turned_step(2, third_of(ys[2], late[:, 2, :]), gather("m1", m1_sb[2], 2), root2, 7)
+        par1 = gather("par", gather_windows[1], 1)
+        m2_picked3 = gather("m2", m2_sb[3], 3)
+        update(1, turned_back(turned1, 5), par1, "m2_sb3")
+        root3 = turned_root(ys[3], m2_picked3, 0, late[:, 3, :], roots[:, 1, :])
+        turned3 = turned_step(3, third_of(ys[3], late[:, 4, :]), gather("m1", m1_sb[3], 3), root3, 1)
+        par2 = gather("par", gather_windows[2], 2)
+        par3 = gather("par", gather_windows[3], 3)
         nc.scalar.copy(scatter_windows[held][:], par_held[:])
-        update(2, turned2, "par_held")
-        update(3, turned3, "step3")
+        update(2, turned_back(turned2, 7), par2, "par_held")
+        update(3, turned_back(turned3, 0), par3, "step3")

@@ -26,7 +26,7 @@ TILES = N // P
 BLOCKS = S // P
 SCALE_ROWS = K // 32
 ROWS_PER_QUADRANT = SCALE_ROWS * QUADRANT // P
-SCALE_FIRST = QUADRANT - SCALE_ROWS
+SCALE_FIRST = P - SCALE_ROWS
 VECTOR_SHARE = 96
 
 
@@ -44,8 +44,7 @@ def tile_picked_sadam_none_p_kernel(tc, x_words, x_scales, w1, par, m1, m2, offs
             return table.rearrange("(p t) u -> t p u", t=TILES)[t]
 
         scale_table = keep.tile([P, T], U8, name="scale_table", align_bytes=64)
-        for first, end in ((0, SCALE_FIRST), (QUADRANT, P // 2), (P // 2, P)):
-            nc.gpsimd.memset(scale_table[first:end, :].bitcast(I32), 0)
+        nc.gpsimd.memset(scale_table[:SCALE_FIRST, :].bitcast(I32), 0)
         x_plane = keep.tile([P, S], U8, name="x_plane", align_bytes=64)
         nc.gpsimd.memset(x_plane[:].bitcast(I32), 0)
         nine = keep.tile([P, 1], F32, name="nine")
@@ -54,7 +53,7 @@ def tile_picked_sadam_none_p_kernel(tc, x_words, x_scales, w1, par, m1, m2, offs
         nc.scalar.activation(third[:], nine[:], ACT.Abs_reciprocal_sqrt)
 
         nc.sync.dma_start(offs_sb[:], offs)
-        nc.sync.dma_start(scale_table[SCALE_FIRST:QUADRANT, :].bitcast(I32), x_scales[0].bitcast(I32))
+        nc.sync.dma_start(scale_table[SCALE_FIRST:, :].bitcast(I32), x_scales[0].bitcast(I32))
         w_raw = keep.tile([P, PACK, N], F32, name="w_raw")
         nc.sync.dma_start(w_raw[:], w1.rearrange("(p j) n -> p j n", j=PACK))
         word_table = keep.tile([P, T], I32, name="word_table", align_bytes=64)
@@ -69,8 +68,8 @@ def tile_picked_sadam_none_p_kernel(tc, x_words, x_scales, w1, par, m1, m2, offs
         gather_windows = [par_held if t == held else scatter_windows[t] for t in range(TILES)]
         tables = {"m2": (m2_sb, m2), "m1": (m1_sb, m1), "par": (gather_windows, par)}
         for name, t in (
-            ("par", 0), ("m2", 1), ("m2", 0), ("m1", 0), ("m2", 2), ("m1", 1),
-            ("m1", 2), ("par", 1), ("m2", 3), ("m1", 3),
+            ("m2", 1), ("m1", 1), ("m2", 0), ("m1", 0), ("par", 0), ("m2", 2), ("m1", 2),
+            ("par", 1), ("m2", 3), ("m1", 3),
             ("par", 2), ("par", 3),
         ):
             tiles, table = tables[name]
@@ -146,14 +145,13 @@ def tile_picked_sadam_none_p_kernel(tc, x_words, x_scales, w1, par, m1, m2, offs
             nc.scalar.activation(y_third, y[:], ACT.Copy, scale=third[:])
             return y_third
 
-        def turned_step(t, y_third, m1_picked, r_turned, number):
+        def turned_step(y_third, m1_picked, r_turned, number, a_copy, slot):
             a_turned = bank(number)
             turn(a_turned, y_third, True, False)
             turn(a_turned, m1_picked, False, True)
-            d_turned = keep.tile([P, S], F32, name="d_turned%d" % t)
-            a_copy = keep.tile([P, S], F32, name="a_copy%d" % t)
-            nc.scalar.copy(a_copy[:], a_turned[:])
-            nc.gpsimd.tensor_tensor(d_turned[:], a_copy[:], r_turned, ALU.mult)
+            d_turned = keep.tile([P, S], F32, name=slot)
+            nc.scalar.copy(a_copy, a_turned[:])
+            nc.gpsimd.tensor_tensor(d_turned[:], a_copy, r_turned, ALU.mult)
             return d_turned
 
         def turned_back(turned, number):
@@ -170,8 +168,8 @@ def tile_picked_sadam_none_p_kernel(tc, x_words, x_scales, w1, par, m1, m2, offs
             nc.sync.dma_start(rows(out, t), scatter_windows[t][:])
 
         ys = [project(t, t) for t in range(TILES)]
-        par0 = gather("par", gather_windows[0], 0)
         m2_picked1 = gather("m2", m2_sb[1], 1)
+        m1_picked1 = gather("m1", m1_sb[1], 1)
         terms0 = keep.tile([P, 2, S], F32, name="terms0")
         nc.scalar.activation(terms0[:, 0, :], ys[0][:], ACT.Square, scale=1.0 / math.sqrt(7.0))
         third_of(ys[0], terms0[:, 1, :])
@@ -183,21 +181,27 @@ def tile_picked_sadam_none_p_kernel(tc, x_words, x_scales, w1, par, m1, m2, offs
         nc.vector.tensor_tensor(a0[:], m1_sb[0][:].indirect(ent_sb[:]), terms0[:, 1, :], ALU.add)
         step0 = keep.tile([P, S], F32, name="step0")
         nc.gpsimd.tensor_tensor(step0[:], a0[:], r0[:], ALU.mult)
+        par0 = gather("par", gather_windows[0], 0)
         m2_picked2 = gather("m2", m2_sb[2], 2)
         update(0, step0, par0, "m2_sb2")
 
         terms1 = keep.tile([P, 2, S], F32, name="terms1")
-        late = keep.tile([P, 5, S], F32, name="step0")
-        roots = keep.tile([P, 2, S], F32, name="roots")
+        late = keep.tile([P, 4, S], F32, name="b0")
+        terms3 = keep.tile([P, 2, S], F32, name="step0")
+        rest = keep.tile([P, 4, S], F32, name="rest")
         root1 = turned_root(ys[1], m2_picked1, 4, terms1[:, 0, :], late[:, 0, :])
-        turned1 = turned_step(1, third_of(ys[1], terms1[:, 1, :]), gather("m1", m1_sb[1], 1), root1, 5)
-        root2 = turned_root(ys[2], m2_picked2, 6, late[:, 1, :], roots[:, 0, :])
-        turned2 = turned_step(2, third_of(ys[2], late[:, 2, :]), gather("m1", m1_sb[2], 2), root2, 7)
+        turned1 = turned_step(third_of(ys[1], terms1[:, 1, :]), m1_picked1, root1, 5, late[:, 1, :], "a0")
+        root2 = turned_root(ys[2], m2_picked2, 6, late[:, 2, :], rest[:, 0, :])
+        turned2 = turned_step(
+            third_of(ys[2], late[:, 3, :]), gather("m1", m1_sb[2], 2), root2, 7, rest[:, 1, :], "turned2"
+        )
         par1 = gather("par", gather_windows[1], 1)
         m2_picked3 = gather("m2", m2_sb[3], 3)
         update(1, turned_back(turned1, 5), par1, "m2_sb3")
-        root3 = turned_root(ys[3], m2_picked3, 0, late[:, 3, :], roots[:, 1, :])
-        turned3 = turned_step(3, third_of(ys[3], late[:, 4, :]), gather("m1", m1_sb[3], 3), root3, 1)
+        root3 = turned_root(ys[3], m2_picked3, 0, terms3[:, 0, :], rest[:, 2, :])
+        turned3 = turned_step(
+            third_of(ys[3], terms3[:, 1, :]), gather("m1", m1_sb[3], 3), root3, 1, rest[:, 3, :], "turned3"
+        )
         par2 = gather("par", gather_windows[2], 2)
         par3 = gather("par", gather_windows[3], 3)
         nc.scalar.copy(scatter_windows[held][:], par_held[:])

@@ -68,8 +68,8 @@ def tile_picked_sadam_none_p_kernel(tc, x_words, x_scales, w1, par, m1, m2, offs
         gather_windows = [par_held if t == held else scatter_windows[t] for t in range(TILES)]
         tables = {"m2": (m2_sb, m2), "m1": (m1_sb, m1), "par": (gather_windows, par)}
         for name, t in (
-            ("m2", 1), ("m1", 1), ("m2", 0), ("m1", 0), ("par", 0), ("m2", 2), ("m1", 2),
-            ("par", 1), ("m2", 3), ("m1", 3),
+            ("par", 0), ("m2", 1), ("m2", 0), ("m1", 0), ("m1", 1), ("m2", 2),
+            ("m1", 2), ("par", 1), ("m2", 3), ("m1", 3),
             ("par", 2), ("par", 3),
         ):
             tiles, table = tables[name]
@@ -159,17 +159,20 @@ def tile_picked_sadam_none_p_kernel(tc, x_words, x_scales, w1, par, m1, m2, offs
             turn(d_bank, turned, True, True)
             return d_bank
 
-        def update(t, step, par_picked, slot):
-            minus_step = keep.tile([P, S], F32, name=slot)
-            nc.scalar.activation(minus_step[:], step[:], ACT.Copy, scale=-1.0)
+        def scatter(t, par_picked, minus_step):
             nc.vector.tensor_tensor(
                 scatter_windows[t][:].indirect(ent_sb[:]), par_picked[:], minus_step[:], ALU.add
             )
             nc.sync.dma_start(rows(out, t), scatter_windows[t][:])
 
+        def update(t, step, par_picked, slot):
+            minus_step = keep.tile([P, S], F32, name=slot)
+            nc.scalar.activation(minus_step[:], step[:], ACT.Copy, scale=-1.0)
+            scatter(t, par_picked, minus_step)
+
         ys = [project(t, t) for t in range(TILES)]
+        par0 = gather("par", gather_windows[0], 0)
         m2_picked1 = gather("m2", m2_sb[1], 1)
-        m1_picked1 = gather("m1", m1_sb[1], 1)
         terms0 = keep.tile([P, 2, S], F32, name="terms0")
         nc.scalar.activation(terms0[:, 0, :], ys[0][:], ACT.Square, scale=1.0 / math.sqrt(7.0))
         third_of(ys[0], terms0[:, 1, :])
@@ -177,30 +180,34 @@ def tile_picked_sadam_none_p_kernel(tc, x_words, x_scales, w1, par, m1, m2, offs
         nc.vector.tensor_tensor(b0[:], m2_sb[0][:].indirect(ent_sb[:]), terms0[:, 0, :], ALU.add)
         r0 = keep.tile([P, S], F32, name="r0")
         nc.scalar.activation(r0[:], b0[:], ACT.Abs_reciprocal_sqrt, scale=0.875 / 0.375**2)
+        minus_r0 = keep.tile([P, S], F32, name="minus_r0")
+        nc.scalar.activation(minus_r0[:], r0[:], ACT.Copy, scale=-1.0)
         a0 = keep.tile([P, S], F32, name="a0")
         nc.vector.tensor_tensor(a0[:], m1_sb[0][:].indirect(ent_sb[:]), terms0[:, 1, :], ALU.add)
-        step0 = keep.tile([P, S], F32, name="step0")
-        nc.gpsimd.tensor_tensor(step0[:], a0[:], r0[:], ALU.mult)
-        par0 = gather("par", gather_windows[0], 0)
+        minus_step0 = keep.tile([P, S], F32, name="step0")
+        nc.gpsimd.tensor_tensor(minus_step0[:], a0[:], minus_r0[:], ALU.mult)
+        m1_picked1 = gather("m1", m1_sb[1], 1)
+        par0_moved = keep.tile([P, S], F32, name="m1_sb1")
+        nc.scalar.copy(par0_moved[:], par0[:])
         m2_picked2 = gather("m2", m2_sb[2], 2)
-        update(0, step0, par0, "m2_sb2")
+        scatter(0, par0_moved, minus_step0)
 
         terms1 = keep.tile([P, 2, S], F32, name="terms1")
-        late = keep.tile([P, 4, S], F32, name="b0")
-        terms3 = keep.tile([P, 2, S], F32, name="step0")
+        late = keep.tile([P, 2, S], F32, name="r0")
+        terms23 = keep.tile([P, 4, S], F32, name="par_picked0")
         rest = keep.tile([P, 4, S], F32, name="rest")
         root1 = turned_root(ys[1], m2_picked1, 4, terms1[:, 0, :], late[:, 0, :])
-        turned1 = turned_step(third_of(ys[1], terms1[:, 1, :]), m1_picked1, root1, 5, late[:, 1, :], "a0")
-        root2 = turned_root(ys[2], m2_picked2, 6, late[:, 2, :], rest[:, 0, :])
+        turned1 = turned_step(third_of(ys[1], terms1[:, 1, :]), m1_picked1, root1, 5, late[:, 1, :], "step0")
+        root2 = turned_root(ys[2], m2_picked2, 6, terms23[:, 0, :], rest[:, 0, :])
         turned2 = turned_step(
-            third_of(ys[2], late[:, 3, :]), gather("m1", m1_sb[2], 2), root2, 7, rest[:, 1, :], "turned2"
+            third_of(ys[2], terms23[:, 1, :]), gather("m1", m1_sb[2], 2), root2, 7, rest[:, 1, :], "turned2"
         )
         par1 = gather("par", gather_windows[1], 1)
         m2_picked3 = gather("m2", m2_sb[3], 3)
         update(1, turned_back(turned1, 5), par1, "m2_sb3")
-        root3 = turned_root(ys[3], m2_picked3, 0, terms3[:, 0, :], rest[:, 2, :])
+        root3 = turned_root(ys[3], m2_picked3, 0, terms23[:, 2, :], rest[:, 2, :])
         turned3 = turned_step(
-            third_of(ys[3], terms3[:, 1, :]), gather("m1", m1_sb[3], 3), root3, 1, rest[:, 3, :], "turned3"
+            third_of(ys[3], terms23[:, 3, :]), gather("m1", m1_sb[3], 3), root3, 1, rest[:, 3, :], "turned3"
         )
         par2 = gather("par", gather_windows[2], 2)
         par3 = gather("par", gather_windows[3], 3)

@@ -43,10 +43,10 @@ def tile_picked_sadam_none_p_kernel(tc, x_words, x_scales, w1, par, m1, m2, offs
         def rows(table, t):
             return table.rearrange("(p t) u -> t p u", t=TILES)[t]
 
-        scale_table = keep.tile([P, T], U8, name="scale_table", align_bytes=64)
-        nc.gpsimd.memset(scale_table[:SCALE_FIRST, :].bitcast(I32), 0)
         x_plane = keep.tile([P, S], U8, name="x_plane", align_bytes=64)
         nc.gpsimd.memset(x_plane[:].bitcast(I32), 0)
+        scale_table = keep.tile([P, T], U8, name="scale_table", align_bytes=64)
+        nc.gpsimd.memset(scale_table[:SCALE_FIRST, :].bitcast(I32), 0)
         nine = keep.tile([P, 1], F32, name="nine")
         nc.vector.memset(nine[:], 9.0)
         third = keep.tile([P, 1], F32, name="third")
@@ -59,6 +59,24 @@ def tile_picked_sadam_none_p_kernel(tc, x_words, x_scales, w1, par, m1, m2, offs
         word_table = keep.tile([P, T], I32, name="word_table", align_bytes=64)
         nc.sync.dma_start(word_table[:], x_words[0].rearrange("p c r -> p (c r)").bitcast(I32))
         nc.sync.dma_start(ent_sb[:], ent)
+
+        ident = keep.tile([P, P], F32, name="ident")
+        make_identity(nc, ident[:])
+
+        x_codes = keep.tile([P, S], U32, name="x_codes", align_bytes=64)
+        scale_picked = keep.tile([P, S], U8, name="scale_picked", align_bytes=64)
+        nc.vector.tensor_copy(scale_picked[:], scale_table[:].indirect(offs_sb[:]))
+        for quadrant in range(P // QUADRANT):
+            source = SCALE_FIRST + ROWS_PER_QUADRANT * quadrant
+            target = QUADRANT * quadrant
+            nc.sync.dma_start(
+                x_plane[target : target + ROWS_PER_QUADRANT, :].bitcast(I32),
+                scale_picked[source : source + ROWS_PER_QUADRANT, :].bitcast(I32),
+            )
+        halves = [slice(h * S // 2, (h + 1) * S // 2) for h in range(2)]
+        for cols in halves:
+            entries = offs_sb[:, cols.start // GROUP : cols.stop // GROUP]
+            nc.vector.tensor_copy(x_codes[:, cols], word_table[:].bitcast(U32).indirect(entries))
 
         m1_sb = [keep.tile([P, U], F32, name="m1_sb%d" % t) for t in range(TILES)]
         m2_sb = [keep.tile([P, U], F32, name="m2_sb%d" % t) for t in range(TILES)]
@@ -74,21 +92,6 @@ def tile_picked_sadam_none_p_kernel(tc, x_words, x_scales, w1, par, m1, m2, offs
         ):
             tiles, table = tables[name]
             nc.sync.dma_start(tiles[t][:], rows(table, t))
-
-        ident = keep.tile([P, P], F32, name="ident")
-        make_identity(nc, ident[:])
-
-        x_codes = keep.tile([P, S], U32, name="x_codes", align_bytes=64)
-        scale_picked = keep.tile([P, S], U8, name="scale_picked", align_bytes=64)
-        nc.vector.tensor_copy(scale_picked[:], scale_table[:].indirect(offs_sb[:]))
-        for quadrant in range(P // QUADRANT):
-            source = SCALE_FIRST + ROWS_PER_QUADRANT * quadrant
-            target = QUADRANT * quadrant
-            nc.scalar.dma_start(
-                x_plane[target : target + ROWS_PER_QUADRANT, :].bitcast(I32),
-                scale_picked[source : source + ROWS_PER_QUADRANT, :].bitcast(I32),
-            )
-        nc.vector.tensor_copy(x_codes[:], word_table[:].bitcast(U32).indirect(offs_sb[:]))
 
         w_grouped = keep.tile([P, N * PACK], BF16, name="w_grouped", align_bytes=64)
         grouped_view = w_grouped[:].rearrange("p (t m j) -> p m t j", t=TILES, j=PACK)
@@ -114,15 +117,15 @@ def tile_picked_sadam_none_p_kernel(tc, x_words, x_scales, w1, par, m1, m2, offs
                     is_transpose=True,
                 )
 
-        def project(t, number):
+        def project(t, number, entries):
             cols = slice(t * P, (t + 1) * P)
-            y = bank(number)
+            y = bank(number)[:, : entries.stop - entries.start]
             nc.tensor.matmul_mx(
-                out=y[:],
+                out=y,
                 lhsT=w_codes[:, cols].bitcast(FP8X4),
                 lhsT_scale=w_plane[:, cols],
-                rhs=x_codes[:].bitcast(FP8X4),
-                rhs_scale=x_plane[:],
+                rhs=x_codes[:, entries].bitcast(FP8X4),
+                rhs_scale=x_plane[:, entries],
                 start=True,
                 stop=True,
             )
@@ -134,7 +137,7 @@ def tile_picked_sadam_none_p_kernel(tc, x_words, x_scales, w1, par, m1, m2, offs
             return picked
 
         def turned_root(y, m2_picked, number, y_square, r_turned):
-            nc.scalar.activation(y_square, y[:], ACT.Square, scale=1.0 / math.sqrt(7.0))
+            nc.scalar.activation(y_square, y, ACT.Square, scale=1.0 / math.sqrt(7.0))
             b_turned = bank(number)
             turn(b_turned, y_square, True, False)
             turn(b_turned, m2_picked, False, True)
@@ -142,7 +145,7 @@ def tile_picked_sadam_none_p_kernel(tc, x_words, x_scales, w1, par, m1, m2, offs
             return r_turned
 
         def third_of(y, y_third):
-            nc.scalar.activation(y_third, y[:], ACT.Copy, scale=third[:])
+            nc.scalar.activation(y_third, y, ACT.Copy, scale=third[:])
             return y_third
 
         def turned_step(y_third, m1_picked, r_turned, number, a_copy, slot):
@@ -170,12 +173,15 @@ def tile_picked_sadam_none_p_kernel(tc, x_words, x_scales, w1, par, m1, m2, offs
             nc.scalar.activation(minus_step[:], step[:], ACT.Copy, scale=-1.0)
             scatter(t, par_picked, minus_step)
 
-        ys = [project(t, t) for t in range(TILES)]
+        y0_halves = [project(0, number, cols) for number, cols in zip((0, BANKS - 1), halves)]
+        ys = [None] + [project(t, t, slice(0, S)) for t in range(1, TILES)]
         par0 = gather("par", gather_windows[0], 0)
         m2_picked1 = gather("m2", m2_sb[1], 1)
         terms0 = keep.tile([P, 2, S], F32, name="terms0")
-        nc.scalar.activation(terms0[:, 0, :], ys[0][:], ACT.Square, scale=1.0 / math.sqrt(7.0))
-        third_of(ys[0], terms0[:, 1, :])
+        for y, cols in zip(y0_halves, halves):
+            nc.scalar.activation(terms0[:, 0, cols], y, ACT.Square, scale=1.0 / math.sqrt(7.0))
+        for y, cols in zip(y0_halves, halves):
+            third_of(y, terms0[:, 1, cols])
         b0 = keep.tile([P, S], F32, name="b0")
         nc.vector.tensor_tensor(b0[:], m2_sb[0][:].indirect(ent_sb[:]), terms0[:, 0, :], ALU.add)
         r0 = keep.tile([P, S], F32, name="r0")

@@ -28,6 +28,8 @@ SCALE_ROWS = K // 32
 ROWS_PER_QUADRANT = SCALE_ROWS * QUADRANT // P
 SCALE_FIRST = P - SCALE_ROWS
 VECTOR_SHARE = 96
+SQUARE_SCALE = 1.0 / math.sqrt(7.0)
+ROOT_SCALE = 0.875 / 0.375**2
 
 
 def tile_picked_sadam_none_p_kernel(tc, x_words, x_scales, w1, par, m1, m2, offs, ent, out):
@@ -52,10 +54,12 @@ def tile_picked_sadam_none_p_kernel(tc, x_words, x_scales, w1, par, m1, m2, offs
         third = keep.tile([P, 1], F32, name="third")
         nc.scalar.activation(third[:], nine[:], ACT.Abs_reciprocal_sqrt)
 
+        w_raw = keep.tile([P, PACK, N], F32, name="w_raw")
+        w_rows = w1.rearrange("(p j) n -> p j n", j=PACK)
+        nc.sync.dma_start(w_raw[:, :1], w_rows[:, :1])
         nc.sync.dma_start(offs_sb[:], offs)
         nc.sync.dma_start(scale_table[SCALE_FIRST:, :].bitcast(I32), x_scales[0].bitcast(I32))
-        w_raw = keep.tile([P, PACK, N], F32, name="w_raw")
-        nc.sync.dma_start(w_raw[:], w1.rearrange("(p j) n -> p j n", j=PACK))
+        nc.sync.dma_start(w_raw[:, 1:], w_rows[:, 1:])
         word_table = keep.tile([P, T], I32, name="word_table", align_bytes=64)
         nc.sync.dma_start(word_table[:], x_words[0].rearrange("p c r -> p (c r)").bitcast(I32))
         nc.sync.dma_start(ent_sb[:], ent)
@@ -137,22 +141,22 @@ def tile_picked_sadam_none_p_kernel(tc, x_words, x_scales, w1, par, m1, m2, offs
             return picked
 
         def turned_root(y, m2_picked, number, y_square, r_turned):
-            nc.scalar.activation(y_square, y, ACT.Square, scale=1.0 / math.sqrt(7.0))
+            nc.scalar.activation(y_square, y, ACT.Square, scale=SQUARE_SCALE)
             b_turned = bank(number)
             turn(b_turned, y_square, True, False)
             turn(b_turned, m2_picked, False, True)
-            nc.scalar.activation(r_turned, b_turned[:], ACT.Abs_reciprocal_sqrt, scale=0.875 / 0.375**2)
+            nc.scalar.activation(r_turned, b_turned[:], ACT.Abs_reciprocal_sqrt, scale=ROOT_SCALE)
             return r_turned
 
         def third_of(y, y_third):
             nc.scalar.activation(y_third, y, ACT.Copy, scale=third[:])
             return y_third
 
-        def turned_step(y_third, m1_picked, r_turned, number, a_copy, slot):
+        def turned_step(y_third, m1_picked, r_turned, number, a_copy, after):
             a_turned = bank(number)
             turn(a_turned, y_third, True, False)
             turn(a_turned, m1_picked, False, True)
-            d_turned = keep.tile([P, S], F32, name=slot)
+            d_turned = keep.tile([P, S], F32, name=after)
             nc.scalar.copy(a_copy, a_turned[:])
             nc.gpsimd.tensor_tensor(d_turned[:], a_copy, r_turned, ALU.mult)
             return d_turned
@@ -168,24 +172,25 @@ def tile_picked_sadam_none_p_kernel(tc, x_words, x_scales, w1, par, m1, m2, offs
             )
             nc.sync.dma_start(rows(out, t), scatter_windows[t][:])
 
-        def update(t, step, par_picked, slot):
-            minus_step = keep.tile([P, S], F32, name=slot)
+        def update(t, step, par_picked, after):
+            minus_step = keep.tile([P, S], F32, name=after)
             nc.scalar.activation(minus_step[:], step[:], ACT.Copy, scale=-1.0)
             scatter(t, par_picked, minus_step)
 
         y0_halves = [project(0, number, cols) for number, cols in zip((0, BANKS - 1), halves)]
         ys = [None] + [project(t, t, slice(0, S)) for t in range(1, TILES)]
+
         par0 = gather("par", gather_windows[0], 0)
         m2_picked1 = gather("m2", m2_sb[1], 1)
         terms0 = keep.tile([P, 2, S], F32, name="terms0")
         for y, cols in zip(y0_halves, halves):
-            nc.scalar.activation(terms0[:, 0, cols], y, ACT.Square, scale=1.0 / math.sqrt(7.0))
+            nc.scalar.activation(terms0[:, 0, cols], y, ACT.Square, scale=SQUARE_SCALE)
         for y, cols in zip(y0_halves, halves):
             third_of(y, terms0[:, 1, cols])
         b0 = keep.tile([P, S], F32, name="b0")
         nc.vector.tensor_tensor(b0[:], m2_sb[0][:].indirect(ent_sb[:]), terms0[:, 0, :], ALU.add)
         r0 = keep.tile([P, S], F32, name="r0")
-        nc.scalar.activation(r0[:], b0[:], ACT.Abs_reciprocal_sqrt, scale=0.875 / 0.375**2)
+        nc.scalar.activation(r0[:], b0[:], ACT.Abs_reciprocal_sqrt, scale=ROOT_SCALE)
         minus_r0 = keep.tile([P, S], F32, name="minus_r0")
         nc.scalar.activation(minus_r0[:], r0[:], ACT.Copy, scale=-1.0)
         a0 = keep.tile([P, S], F32, name="a0")
@@ -199,21 +204,23 @@ def tile_picked_sadam_none_p_kernel(tc, x_words, x_scales, w1, par, m1, m2, offs
         scatter(0, par0_moved, minus_step0)
 
         terms1 = keep.tile([P, 2, S], F32, name="terms1")
-        late = keep.tile([P, 2, S], F32, name="r0")
+        factors1 = keep.tile([P, 2, S], F32, name="r0")
         terms23 = keep.tile([P, 4, S], F32, name="par_picked0")
-        rest = keep.tile([P, 4, S], F32, name="rest")
-        root1 = turned_root(ys[1], m2_picked1, 4, terms1[:, 0, :], late[:, 0, :])
-        turned1 = turned_step(third_of(ys[1], terms1[:, 1, :]), m1_picked1, root1, 5, late[:, 1, :], "step0")
-        root2 = turned_root(ys[2], m2_picked2, 6, terms23[:, 0, :], rest[:, 0, :])
+        factors23 = keep.tile([P, 4, S], F32, name="factors23")
+        root1 = turned_root(ys[1], m2_picked1, 4, terms1[:, 0, :], factors1[:, 0, :])
+        turned1 = turned_step(
+            third_of(ys[1], terms1[:, 1, :]), m1_picked1, root1, 5, factors1[:, 1, :], "step0"
+        )
+        root2 = turned_root(ys[2], m2_picked2, 6, terms23[:, 0, :], factors23[:, 0, :])
         turned2 = turned_step(
-            third_of(ys[2], terms23[:, 1, :]), gather("m1", m1_sb[2], 2), root2, 7, rest[:, 1, :], "turned2"
+            third_of(ys[2], terms23[:, 1, :]), gather("m1", m1_sb[2], 2), root2, 7, factors23[:, 1, :], "turned2"
         )
         par1 = gather("par", gather_windows[1], 1)
         m2_picked3 = gather("m2", m2_sb[3], 3)
         update(1, turned_back(turned1, 5), par1, "m2_sb3")
-        root3 = turned_root(ys[3], m2_picked3, 0, terms23[:, 2, :], rest[:, 2, :])
+        root3 = turned_root(ys[3], m2_picked3, 0, terms23[:, 2, :], factors23[:, 2, :])
         turned3 = turned_step(
-            third_of(ys[3], terms23[:, 3, :]), gather("m1", m1_sb[3], 3), root3, 1, rest[:, 3, :], "turned3"
+            third_of(ys[3], terms23[:, 3, :]), gather("m1", m1_sb[3], 3), root3, 1, factors23[:, 3, :], "turned3"
         )
         par2 = gather("par", gather_windows[2], 2)
         par3 = gather("par", gather_windows[3], 3)

@@ -28,6 +28,7 @@ SCALE_ROWS = K // 32
 ROWS_PER_QUADRANT = SCALE_ROWS * QUADRANT // P
 SCALE_FIRST = P - SCALE_ROWS
 VECTOR_SHARE = 96
+W_FIRST = 256
 SQUARE_SCALE = 1.0 / math.sqrt(7.0)
 ROOT_SCALE = 0.875 / 0.375**2
 
@@ -55,11 +56,12 @@ def tile_picked_sadam_none_p_kernel(tc, x_words, x_scales, w1, par, m1, m2, offs
         nc.scalar.activation(third[:], nine[:], ACT.Abs_reciprocal_sqrt)
 
         w_raw = keep.tile([P, PACK, N], F32, name="w_raw")
-        w_rows = w1.rearrange("(p j) n -> p j n", j=PACK)
-        nc.sync.dma_start(w_raw[:, :1], w_rows[:, :1])
+        w_rows = w1.rearrange("(p j) n -> p (j n)", j=PACK)
+        w_flat = w_raw[:].rearrange("p j n -> p (j n)")
+        nc.sync.dma_start(w_flat[:, :W_FIRST], w_rows[:, :W_FIRST])
         nc.sync.dma_start(offs_sb[:], offs)
         nc.sync.dma_start(scale_table[SCALE_FIRST:, :].bitcast(I32), x_scales[0].bitcast(I32))
-        nc.sync.dma_start(w_raw[:, 1:], w_rows[:, 1:])
+        nc.sync.dma_start(w_flat[:, W_FIRST:], w_rows[:, W_FIRST:])
         word_table = keep.tile([P, T], I32, name="word_table", align_bytes=64)
         nc.sync.dma_start(word_table[:], x_words[0].rearrange("p c r -> p (c r)").bitcast(I32))
         nc.sync.dma_start(ent_sb[:], ent)
@@ -73,7 +75,8 @@ def tile_picked_sadam_none_p_kernel(tc, x_words, x_scales, w1, par, m1, m2, offs
         for quadrant in range(P // QUADRANT):
             source = SCALE_FIRST + ROWS_PER_QUADRANT * quadrant
             target = QUADRANT * quadrant
-            nc.sync.dma_start(
+            queue = nc.scalar if quadrant % 2 else nc.sync
+            queue.dma_start(
                 x_plane[target : target + ROWS_PER_QUADRANT, :].bitcast(I32),
                 scale_picked[source : source + ROWS_PER_QUADRANT, :].bitcast(I32),
             )

@@ -54,6 +54,8 @@ def tile_picked_sadam_none_p_kernel(tc, x_words, x_scales, w1, par, m1, m2, offs
         nc.vector.memset(nine[:], 9.0)
         third = keep.tile([P, 1], F32, name="third")
         nc.scalar.activation(third[:], nine[:], ACT.Abs_reciprocal_sqrt)
+        minus_third = keep.tile([P, 1], F32, name="minus_third")
+        nc.scalar.activation(minus_third[:], third[:], ACT.Copy, scale=-1.0)
 
         w_raw = keep.tile([P, PACK, N], F32, name="w_raw")
         w_rows = w1.rearrange("(p j) n -> p (j n)", j=PACK)
@@ -82,23 +84,16 @@ def tile_picked_sadam_none_p_kernel(tc, x_words, x_scales, w1, par, m1, m2, offs
             )
         halves = [slice(h * S // 2, (h + 1) * S // 2) for h in range(2)]
         for cols in halves:
-            entries = offs_sb[:, cols.start // GROUP : cols.stop // GROUP]
-            nc.vector.tensor_copy(x_codes[:, cols], word_table[:].bitcast(U32).indirect(entries))
+            picks = offs_sb[:, cols.start // GROUP : cols.stop // GROUP]
+            nc.vector.tensor_copy(x_codes[:, cols], word_table[:].bitcast(U32).indirect(picks))
 
-        m1_sb = [keep.tile([P, U], F32, name="m1_sb%d" % t) for t in range(TILES)]
         m2_sb = [keep.tile([P, U], F32, name="m2_sb%d" % t) for t in range(TILES)]
-        scatter_windows = [keep.tile([P, U], F32, name="par_sb%d" % t) for t in range(TILES)]
-        held = TILES - 2
-        par_held = keep.tile([P, U], F32, name="par_held")
-        gather_windows = [par_held if t == held else scatter_windows[t] for t in range(TILES)]
-        tables = {"m2": (m2_sb, m2), "m1": (m1_sb, m1), "par": (gather_windows, par)}
-        for name, t in (
-            ("par", 0), ("m2", 1), ("m2", 0), ("m1", 0), ("m1", 1), ("m2", 2),
-            ("m1", 2), ("par", 1), ("m2", 3), ("m1", 3),
-            ("par", 2), ("par", 3),
-        ):
-            tiles, table = tables[name]
-            nc.sync.dma_start(tiles[t][:], rows(table, t))
+        m1_sb = [keep.tile([P, U], F32, name="m1_sb%d" % t) for t in range(TILES)]
+        par_sb = [keep.tile([P, U], F32, name="par_sb%d" % t) for t in range(TILES)]
+        for t in range(TILES):
+            moments = [(m2_sb, m2), (m1_sb, m1)]
+            for tiles, table in (moments if t else moments[::-1]) + [(par_sb, par)]:
+                nc.sync.dma_start(tiles[t][:], rows(table, t))
 
         w_grouped = keep.tile([P, N * PACK], BF16, name="w_grouped", align_bytes=64)
         grouped_view = w_grouped[:].rearrange("p (t m j) -> p m t j", t=TILES, j=PACK)
@@ -124,109 +119,83 @@ def tile_picked_sadam_none_p_kernel(tc, x_words, x_scales, w1, par, m1, m2, offs
                     is_transpose=True,
                 )
 
-        def project(t, number, entries):
+        def project(t, number, picks):
             cols = slice(t * P, (t + 1) * P)
-            y = bank(number)[:, : entries.stop - entries.start]
+            y = bank(number)[:, : picks.stop - picks.start]
             nc.tensor.matmul_mx(
                 out=y,
                 lhsT=w_codes[:, cols].bitcast(FP8X4),
                 lhsT_scale=w_plane[:, cols],
-                rhs=x_codes[:, entries].bitcast(FP8X4),
-                rhs_scale=x_plane[:, entries],
+                rhs=x_codes[:, picks].bitcast(FP8X4),
+                rhs_scale=x_plane[:, picks],
                 start=True,
                 stop=True,
             )
             return y
 
-        def gather(name, window, t):
-            picked = keep.tile([P, S], F32, name="%s_picked%d" % (name, t))
-            nc.vector.tensor_copy(picked[:], window[:].indirect(ent_sb[:]))
-            return picked
+        def entries(cols):
+            return ent_sb[:, cols.start // GROUP : cols.stop // GROUP]
 
-        def turned_root(y, m2_picked, number, y_square, r_turned):
-            nc.scalar.activation(y_square, y, ACT.Square, scale=SQUARE_SCALE)
-            b_turned = bank(number)
-            turn(b_turned, y_square, True, False)
-            turn(b_turned, m2_picked, False, True)
-            nc.scalar.activation(r_turned, b_turned[:], ACT.Abs_reciprocal_sqrt, scale=ROOT_SCALE)
-            return r_turned
+        def gather(picked, window, cols):
+            nc.scalar.activation(picked[:, cols], window[:].indirect(entries(cols)), ACT.Copy)
 
-        def third_of(y, y_third):
-            nc.scalar.activation(y_third, y, ACT.Copy, scale=third[:])
-            return y_third
-
-        def turned_step(y_third, m1_picked, r_turned, number, a_copy, after):
-            a_turned = bank(number)
-            turn(a_turned, y_third, True, False)
-            turn(a_turned, m1_picked, False, True)
-            d_turned = keep.tile([P, S], F32, name=after)
-            nc.scalar.copy(a_copy, a_turned[:])
-            nc.gpsimd.tensor_tensor(d_turned[:], a_copy, r_turned, ALU.mult)
-            return d_turned
-
-        def turned_back(turned, number):
-            d_bank = bank(number)
-            turn(d_bank, turned, True, True)
-            return d_bank
-
-        def scatter(t, par_picked, minus_step):
+        def scatter(t, par_picked, minus_step, cols):
             nc.vector.tensor_tensor(
-                scatter_windows[t][:].indirect(ent_sb[:]), par_picked[:], minus_step[:], ALU.add
+                par_sb[t][:].indirect(entries(cols)), par_picked[:, cols], minus_step[:, cols], ALU.add
             )
-            nc.sync.dma_start(rows(out, t), scatter_windows[t][:])
 
-        def update(t, step, par_picked, after):
-            minus_step = keep.tile([P, S], F32, name=after)
-            nc.scalar.activation(minus_step[:], step[:], ACT.Copy, scale=-1.0)
-            scatter(t, par_picked, minus_step)
+        def work(name, t):
+            return keep.tile([P, S], F32, name="%s%d" % (name, t))
 
+        whole = slice(0, S)
         y0_halves = [project(0, number, cols) for number, cols in zip((0, BANKS - 1), halves)]
-        ys = [None] + [project(t, t, slice(0, S)) for t in range(1, TILES)]
+        ys = [None] + [project(t, t, whole) for t in range(1, TILES)]
 
-        par0 = gather("par", gather_windows[0], 0)
-        m2_picked1 = gather("m2", m2_sb[1], 1)
-        terms0 = keep.tile([P, 2, S], F32, name="terms0")
-        for y, cols in zip(y0_halves, halves):
-            nc.scalar.activation(terms0[:, 0, cols], y, ACT.Square, scale=SQUARE_SCALE)
-        for y, cols in zip(y0_halves, halves):
-            third_of(y, terms0[:, 1, cols])
-        b0 = keep.tile([P, S], F32, name="b0")
-        nc.vector.tensor_tensor(b0[:], m2_sb[0][:].indirect(ent_sb[:]), terms0[:, 0, :], ALU.add)
-        r0 = keep.tile([P, S], F32, name="r0")
-        nc.scalar.activation(r0[:], b0[:], ACT.Abs_reciprocal_sqrt, scale=ROOT_SCALE)
-        minus_r0 = keep.tile([P, S], F32, name="minus_r0")
-        nc.scalar.activation(minus_r0[:], r0[:], ACT.Copy, scale=-1.0)
-        a0 = keep.tile([P, S], F32, name="a0")
-        nc.vector.tensor_tensor(a0[:], m1_sb[0][:].indirect(ent_sb[:]), terms0[:, 1, :], ALU.add)
-        minus_step0 = keep.tile([P, S], F32, name="step0")
-        nc.gpsimd.tensor_tensor(minus_step0[:], a0[:], minus_r0[:], ALU.mult)
-        m1_picked1 = gather("m1", m1_sb[1], 1)
-        par0_moved = keep.tile([P, S], F32, name="m1_sb1")
-        nc.scalar.copy(par0_moved[:], par0[:])
-        m2_picked2 = gather("m2", m2_sb[2], 2)
-        scatter(0, par0_moved, minus_step0)
+        def first_moment(minus_a, y, m1_picked):
+            nc.vector.scalar_tensor_tensor(minus_a, y, minus_third[:], m1_picked, ALU.mult, ALU.subtract)
 
-        terms1 = keep.tile([P, 2, S], F32, name="terms1")
-        factors1 = keep.tile([P, 2, S], F32, name="r0")
-        terms23 = keep.tile([P, 4, S], F32, name="par_picked0")
-        factors23 = keep.tile([P, 4, S], F32, name="factors23")
-        root1 = turned_root(ys[1], m2_picked1, 4, terms1[:, 0, :], factors1[:, 0, :])
-        turned1 = turned_step(
-            third_of(ys[1], terms1[:, 1, :]), m1_picked1, root1, 5, factors1[:, 1, :], "step0"
+        m1_picked, b_sum, root, minus_step, par_picked = (
+            work(name, 0) for name in ("m1_picked", "b_sum", "root", "minus_step", "par_picked")
         )
-        root2 = turned_root(ys[2], m2_picked2, 6, terms23[:, 0, :], factors23[:, 0, :])
-        turned2 = turned_step(
-            third_of(ys[2], terms23[:, 1, :]), gather("m1", m1_sb[2], 2), root2, 7, factors23[:, 1, :], "turned2"
-        )
-        par1 = gather("par", gather_windows[1], 1)
-        m2_picked3 = gather("m2", m2_sb[3], 3)
-        update(1, turned_back(turned1, 5), par1, "m2_sb3")
-        root3 = turned_root(ys[3], m2_picked3, 0, terms23[:, 2, :], factors23[:, 2, :])
-        turned3 = turned_step(
-            third_of(ys[3], terms23[:, 3, :]), gather("m1", m1_sb[3], 3), root3, 1, factors23[:, 3, :], "turned3"
-        )
-        par2 = gather("par", gather_windows[2], 2)
-        par3 = gather("par", gather_windows[3], 3)
-        nc.scalar.copy(scatter_windows[held][:], par_held[:])
-        update(2, turned_back(turned2, 7), par2, "par_held")
-        update(3, turned_back(turned3, 0), par3, "step3")
+        nc.vector.tensor_copy(m1_picked[:], m1_sb[0][:].indirect(ent_sb[:]))
+        for h, (y, cols) in enumerate(zip(y0_halves, halves)):
+            square = keep.tile([P, S // 2], F32, name="square_half%d" % h)
+            nc.scalar.activation(square[:], y, ACT.Square, scale=SQUARE_SCALE)
+            nc.vector.tensor_tensor(b_sum[:, cols], m2_sb[0][:].indirect(entries(cols)), square[:], ALU.add)
+            nc.scalar.activation(root[:, cols], b_sum[:, cols], ACT.Abs_reciprocal_sqrt, scale=ROOT_SCALE)
+        minus_a = keep.tile([P, S], F32, name="square_half0")
+        for y, cols in zip(y0_halves, halves):
+            first_moment(minus_a[:, cols], y, m1_picked[:, cols])
+        for cols in halves:
+            nc.vector.tensor_tensor(minus_step[:, cols], minus_a[:, cols], root[:, cols], ALU.mult)
+            gather(par_picked, par_sb[0], cols)
+        for cols in halves:
+            scatter(0, par_picked, minus_step, cols)
+        nc.sync.dma_start(rows(out, 0), par_sb[0][:])
+
+        for t, (b_bank, root_bank) in zip(range(1, TILES), ((4, 0), (5, 7), (6, 4))):
+            if t < TILES - 1:
+                square = work("square", t)
+                m2_picked = work("terms", t)
+            else:
+                terms = keep.tile([P, 2, S], F32, name="terms%d" % t)
+                square, m2_picked = terms[:, 0, :], terms[:, 1, :]
+            m1_picked, minus_a, minus_step = (work(name, t) for name in ("m1_picked", "minus_a", "minus_step"))
+            nc.scalar.activation(square[:], ys[t], ACT.Square, scale=SQUARE_SCALE)
+            gather(m2_picked, m2_sb[t], whole)
+            b_turned = bank(b_bank)
+            turn(b_turned, square, True, False)
+            turn(b_turned, m2_picked, False, True)
+            gather(m1_picked, m1_sb[t], whole)
+            root_turned = work("terms", t + 1)
+            nc.scalar.activation(root_turned[:], b_turned[:], ACT.Abs_reciprocal_sqrt, scale=ROOT_SCALE)
+            root = bank(root_bank)
+            turn(root, root_turned, True, True)
+            par_picked = work("terms", t)
+            gather(par_picked, par_sb[t], whole)
+            for cols in halves:
+                first_moment(minus_a[:, cols], ys[t][:, cols], m1_picked[:, cols])
+            for cols in halves:
+                nc.vector.tensor_tensor(minus_step[:, cols], root[:, cols], minus_a[:, cols], ALU.mult)
+            scatter(t, par_picked, minus_step, whole)
+            nc.sync.dma_start(rows(out, t), par_sb[t][:])

@@ -90,10 +90,15 @@ def tile_picked_sadam_none_p_kernel(tc, x_words, x_scales, w1, par, m1, m2, offs
         m2_sb = [keep.tile([P, U], F32, name="m2_sb%d" % t) for t in range(TILES)]
         m1_sb = [keep.tile([P, U], F32, name="m1_sb%d" % t) for t in range(TILES)]
         par_sb = [keep.tile([P, U], F32, name="par_sb%d" % t) for t in range(TILES)]
-        for t in range(TILES):
-            moments = [(m2_sb, m2), (m1_sb, m1)]
-            for tiles, table in (moments if t else moments[::-1]) + [(par_sb, par)]:
-                nc.sync.dma_start(tiles[t][:], rows(table, t))
+        tables = {"m2": (m2_sb, m2), "m1": (m1_sb, m1), "par": (par_sb, par)}
+        for name, t in (
+            ("m1", 0), ("m2", 0), ("par", 0),
+            ("m2", 1), ("m1", 1), ("m1", 2), ("par", 1),
+            ("m2", 2), ("m1", 3), ("par", 2),
+            ("m2", 3), ("par", 3),
+        ):
+            tiles, table = tables[name]
+            nc.sync.dma_start(tiles[t][:], rows(table, t))
 
         w_grouped = keep.tile([P, N * PACK], BF16, name="w_grouped", align_bytes=64)
         grouped_view = w_grouped[:].rearrange("p (t m j) -> p m t j", t=TILES, j=PACK)
@@ -107,15 +112,16 @@ def tile_picked_sadam_none_p_kernel(tc, x_words, x_scales, w1, par, m1, m2, offs
         def bank(number):
             return psum.tile([P, S], F32, name="bank%d" % number)
 
-        def turn(target, source, start, stop):
-            for c in range(BLOCKS):
+        def turn(target, source, start, stop, part):
+            blocks = range(part.start // P, part.stop // P)
+            for c in blocks:
                 cols = slice(c * P, (c + 1) * P)
                 nc.tensor.matmul(
                     target[:, cols],
                     source[:, cols],
                     ident[:],
-                    start=start and c == 0,
-                    stop=stop and c == BLOCKS - 1,
+                    start=start and c == blocks[0],
+                    stop=stop and c == blocks[-1],
                     is_transpose=True,
                 )
 
@@ -167,35 +173,77 @@ def tile_picked_sadam_none_p_kernel(tc, x_words, x_scales, w1, par, m1, m2, offs
         for y, cols in zip(y0_halves, halves):
             first_moment(minus_a[:, cols], y, m1_picked[:, cols])
         for cols in halves:
-            nc.vector.tensor_tensor(minus_step[:, cols], minus_a[:, cols], root[:, cols], ALU.mult)
-            gather(par_picked, par_sb[0], cols)
-        for cols in halves:
-            scatter(0, par_picked, minus_step, cols)
+            nc.gpsimd.tensor_tensor(minus_step[:, cols], minus_a[:, cols], root[:, cols], ALU.mult)
+        nc.vector.tensor_copy(par_picked[:], par_sb[0][:].indirect(ent_sb[:]))
+        scatter(0, par_picked, minus_step, whole)
         nc.sync.dma_start(rows(out, 0), par_sb[0][:])
 
-        for t, (b_bank, root_bank) in zip(range(1, TILES), ((4, 0), (5, 7), (6, 4))):
-            if t < TILES - 1:
-                square = work("square", t)
-                m2_picked = work("terms", t)
-            else:
-                terms = keep.tile([P, 2, S], F32, name="terms%d" % t)
-                square, m2_picked = terms[:, 0, :], terms[:, 1, :]
-            m1_picked, minus_a, minus_step = (work(name, t) for name in ("m1_picked", "minus_a", "minus_step"))
-            nc.scalar.activation(square[:], ys[t], ACT.Square, scale=SQUARE_SCALE)
-            gather(m2_picked, m2_sb[t], whole)
-            b_turned = bank(b_bank)
-            turn(b_turned, square, True, False)
-            turn(b_turned, m2_picked, False, True)
-            gather(m1_picked, m1_sb[t], whole)
-            root_turned = work("terms", t + 1)
-            nc.scalar.activation(root_turned[:], b_turned[:], ACT.Abs_reciprocal_sqrt, scale=ROOT_SCALE)
-            root = bank(root_bank)
-            turn(root, root_turned, True, True)
-            par_picked = work("terms", t)
-            gather(par_picked, par_sb[t], whole)
-            for cols in halves:
-                first_moment(minus_a[:, cols], ys[t][:, cols], m1_picked[:, cols])
-            for cols in halves:
-                nc.vector.tensor_tensor(minus_step[:, cols], root[:, cols], minus_a[:, cols], ALU.mult)
+        def picked(table, t, tile, cols):
+            gather(tile, table[t], cols)
+            return tile
+
+        def square_of(t, tile):
+            nc.scalar.activation(tile[:], ys[t], ACT.Square, scale=SQUARE_SCALE)
+            return tile
+
+        def turned_sum(number, square, m2_picked, cols):
+            b_turned = bank(number)
+            turn(b_turned, square, True, False, cols)
+            turn(b_turned, m2_picked, False, True, cols)
+            return b_turned
+
+        def root_of(b_turned, root_turned, number, cols):
+            nc.scalar.activation(
+                root_turned[:, cols], b_turned[:, cols], ACT.Abs_reciprocal_sqrt, scale=ROOT_SCALE
+            )
+            root = bank(number)
+            turn(root, root_turned, True, True, cols)
+            return root
+
+        def product(minus_step, root, minus_a, cols):
+            nc.vector.tensor_tensor(minus_step[:, cols], root[:, cols], minus_a[:, cols], ALU.mult)
+
+        def update(t, par_picked, minus_step):
             scatter(t, par_picked, minus_step, whole)
             nc.sync.dma_start(rows(out, t), par_sb[t][:])
+
+        square1 = square_of(1, work("square", 1))
+        square2 = square_of(2, work("square", 2))
+        b1 = turned_sum(4, square1, picked(m2_sb, 1, work("m2_picked", 1), whole), whole)
+        m1_picked1 = picked(m1_sb, 1, work("m1_picked", 1), whole)
+        root1 = root_of(b1, work("root_turned", 1), 0, whole)
+        after_root1 = keep.tile([P, 2, S], F32, name="m2_picked1")
+        m1_picked2 = picked(m1_sb, 2, after_root1[:, 0, :], whole)
+        par1 = picked(par_sb, 1, after_root1[:, 1, :], whole)
+        minus_a1, step1 = work("minus_a", 1), work("minus_step", 1)
+        for cols in halves:
+            first_moment(minus_a1[:, cols], ys[1][:, cols], m1_picked1[:, cols])
+        for cols in halves:
+            product(step1, root1, minus_a1, cols)
+        minus_a2 = work("root_turned", 1)
+        first_moment(minus_a2[:], ys[2], m1_picked2)
+        update(1, par1, step1)
+
+        b2 = turned_sum(5, square2, picked(m2_sb, 2, work("square", 1), whole), whole)
+        m1_picked3 = picked(m1_sb, 3, work("m1_picked", 3), whole)
+        root2 = root_of(b2, work("root_turned", 2), 7, whole)
+        par2 = picked(par_sb, 2, work("square", 1), whole)
+        step2 = work("minus_step", 2)
+        product(step2, root2, minus_a2, whole)
+        terms3 = keep.tile([P, 2, S], F32, name="root_turned2")
+        minus_a3 = terms3[:, 0, :]
+        first_moment(minus_a3, ys[3], m1_picked3[:])
+        update(2, par2, step2)
+
+        square3 = square_of(3, terms3[:, 1, :])
+        m2_picked3 = work("square", 2)
+        root_turned3, step3 = (work(name, 3) for name in ("root_turned", "minus_step"))
+        b3 = [
+            turned_sum(number, square3, picked(m2_sb, 3, m2_picked3, cols), cols)
+            for number, cols in zip((6, 4), halves)
+        ]
+        root3 = [root_of(b, root_turned3, number, cols) for b, number, cols in zip(b3, (0, 5), halves)]
+        par3 = picked(par_sb, 3, work("square", 2), whole)
+        for root, cols in zip(root3, halves):
+            product(step3, root, minus_a3, cols)
+        update(3, par3, step3)

@@ -50,12 +50,10 @@ def tile_picked_sadam_none_p_kernel(tc, x_words, x_scales, w1, par, m1, m2, offs
         nc.gpsimd.memset(x_plane[:].bitcast(I32), 0)
         scale_table = keep.tile([P, T], U8, name="scale_table", align_bytes=64)
         nc.gpsimd.memset(scale_table[:SCALE_FIRST, :].bitcast(I32), 0)
-        nine = keep.tile([P, 1], F32, name="nine")
-        nc.vector.memset(nine[:], 9.0)
-        third = keep.tile([P, 1], F32, name="third")
-        nc.scalar.activation(third[:], nine[:], ACT.Abs_reciprocal_sqrt)
-        minus_third = keep.tile([P, 1], F32, name="minus_third")
-        nc.scalar.activation(minus_third[:], third[:], ACT.Copy, scale=-1.0)
+        seven = keep.tile([P, 1], F32, name="seven")
+        nc.vector.memset(seven[:], 7.0)
+        first_scale = keep.tile([P, 1], F32, name="first_scale")
+        nc.scalar.activation(first_scale[:], seven[:], ACT.Abs_reciprocal_sqrt)
 
         w_raw = keep.tile([P, PACK, N], F32, name="w_raw")
         w_rows = w1.rearrange("(p j) n -> p (j n)", j=PACK)
@@ -158,7 +156,7 @@ def tile_picked_sadam_none_p_kernel(tc, x_words, x_scales, w1, par, m1, m2, offs
         ys = [None] + [project(t, t, whole) for t in range(1, TILES)]
 
         def first_moment(minus_a, y, m1_picked):
-            nc.vector.scalar_tensor_tensor(minus_a, y, minus_third[:], m1_picked, ALU.mult, ALU.subtract)
+            nc.vector.scalar_tensor_tensor(minus_a, y, -1.0 / 3.0, m1_picked, ALU.mult, ALU.subtract)
 
         m1_picked, b_sum, root, minus_step, par_picked = (
             work(name, 0) for name in ("m1_picked", "b_sum", "root", "minus_step", "par_picked")
@@ -166,7 +164,7 @@ def tile_picked_sadam_none_p_kernel(tc, x_words, x_scales, w1, par, m1, m2, offs
         nc.vector.tensor_copy(m1_picked[:], m1_sb[0][:].indirect(ent_sb[:]))
         for h, (y, cols) in enumerate(zip(y0_halves, halves)):
             square = keep.tile([P, S // 2], F32, name="square_half%d" % h)
-            nc.scalar.activation(square[:], y, ACT.Square, scale=SQUARE_SCALE)
+            nc.scalar.activation(square[:], y, ACT.Square, scale=SQUARE_SCALE if h else first_scale[:])
             nc.vector.tensor_tensor(b_sum[:, cols], m2_sb[0][:].indirect(entries(cols)), square[:], ALU.add)
             nc.scalar.activation(root[:, cols], b_sum[:, cols], ACT.Abs_reciprocal_sqrt, scale=ROOT_SCALE)
         minus_a = keep.tile([P, S], F32, name="square_half0")
@@ -227,23 +225,24 @@ def tile_picked_sadam_none_p_kernel(tc, x_words, x_scales, w1, par, m1, m2, offs
         b2 = turned_sum(5, square2, picked(m2_sb, 2, work("square", 1), whole), whole)
         m1_picked3 = picked(m1_sb, 3, work("m1_picked", 3), whole)
         root2 = root_of(b2, work("root_turned", 2), 7, whole)
-        par2 = picked(par_sb, 2, work("square", 1), whole)
+        after_root2 = keep.tile([P, 3, S], F32, name="square1")
+        par2 = picked(par_sb, 2, after_root2[:, 0, :], whole)
         step2 = work("minus_step", 2)
         product(step2, root2, minus_a2, whole)
-        terms3 = keep.tile([P, 2, S], F32, name="root_turned2")
-        minus_a3 = terms3[:, 0, :]
-        first_moment(minus_a3, ys[3], m1_picked3[:])
+        square3 = square_of(3, after_root2[:, 1, :])
+        minus_a3 = work("root_turned", 2)
+        first_moment(minus_a3[:], ys[3], m1_picked3[:])
         update(2, par2, step2)
 
-        square3 = square_of(3, terms3[:, 1, :])
-        m2_picked3 = work("square", 2)
+        m2_picked3 = after_root2[:, 2, :]
         root_turned3, step3 = (work(name, 3) for name in ("root_turned", "minus_step"))
         b3 = [
             turned_sum(number, square3, picked(m2_sb, 3, m2_picked3, cols), cols)
             for number, cols in zip((6, 4), halves)
         ]
+        par3 = picked(par_sb, 3, work("par_picked", 3), halves[0])
         root3 = [root_of(b, root_turned3, number, cols) for b, number, cols in zip(b3, (0, 5), halves)]
-        par3 = picked(par_sb, 3, work("square", 2), whole)
+        picked(par_sb, 3, par3, halves[1])
         for root, cols in zip(root3, halves):
             product(step3, root, minus_a3, cols)
         update(3, par3, step3)

@@ -222,26 +222,30 @@ def tile_picked_sadam_none_p_kernel(tc, x_words, x_scales, w1, par, m1, m2, offs
         first_moment(minus_a2[:], ys[2], m1_picked2)
         update(1, par1, step1)
 
-        b2 = turned_sum(5, square2, picked(m2_sb, 2, work("square", 1), whole), whole)
-        m1_picked3 = picked(m1_sb, 3, work("m1_picked", 3), whole)
-        root2 = root_of(b2, work("root_turned", 2), 7, whole)
+        m2_picked2, root_turned2, step2 = work("square", 1), work("root_turned", 2), work("minus_step", 2)
+        b2 = [
+            turned_sum(number, square2, picked(m2_sb, 2, m2_picked2, cols), cols)
+            for number, cols in zip((5, 6), halves)
+        ]
+        square3 = square_of(3, work("m2_sb", 2))
+        root2 = [root_of(b, root_turned2, number, cols) for b, number, cols in zip(b2, (7, 4), halves)]
         after_root2 = keep.tile([P, 3, S], F32, name="square1")
+        m1_picked3 = picked(m1_sb, 3, after_root2[:, 1, :], whole)
         par2 = picked(par_sb, 2, after_root2[:, 0, :], whole)
-        step2 = work("minus_step", 2)
-        product(step2, root2, minus_a2, whole)
-        square3 = square_of(3, after_root2[:, 1, :])
+        for root, cols in zip(root2, halves):
+            product(step2, root, minus_a2, cols)
         minus_a3 = work("root_turned", 2)
-        first_moment(minus_a3[:], ys[3], m1_picked3[:])
+        first_moment(minus_a3[:], ys[3], m1_picked3)
         update(2, par2, step2)
 
         m2_picked3 = after_root2[:, 2, :]
         root_turned3, step3 = (work(name, 3) for name in ("root_turned", "minus_step"))
         b3 = [
             turned_sum(number, square3, picked(m2_sb, 3, m2_picked3, cols), cols)
-            for number, cols in zip((6, 4), halves)
+            for number, cols in zip((0, 5), halves)
         ]
         par3 = picked(par_sb, 3, work("par_picked", 3), halves[0])
-        root3 = [root_of(b, root_turned3, number, cols) for b, number, cols in zip(b3, (0, 5), halves)]
+        root3 = [root_of(b, root_turned3, number, cols) for b, number, cols in zip(b3, (6, 1), halves)]
         picked(par_sb, 3, par3, halves[1])
         for root, cols in zip(root3, halves):
             product(step3, root, minus_a3, cols)

@@ -158,8 +158,8 @@ def tile_picked_sadam_none_p_kernel(tc, x_words, x_scales, w1, par, m1, m2, offs
         def first_moment(minus_a, y, m1_picked):
             nc.vector.scalar_tensor_tensor(minus_a, y, -1.0 / 3.0, m1_picked, ALU.mult, ALU.subtract)
 
-        m1_picked, b_sum, root, minus_step, par_picked = (
-            work(name, 0) for name in ("m1_picked", "b_sum", "root", "minus_step", "par_picked")
+        m1_picked, b_sum, root, minus_step = (
+            work(name, 0) for name in ("m1_picked", "b_sum", "root", "minus_step")
         )
         nc.vector.tensor_copy(m1_picked[:], m1_sb[0][:].indirect(ent_sb[:]))
         for h, (y, cols) in enumerate(zip(y0_halves, halves)):
@@ -170,9 +170,12 @@ def tile_picked_sadam_none_p_kernel(tc, x_words, x_scales, w1, par, m1, m2, offs
         minus_a = keep.tile([P, S], F32, name="square_half0")
         for y, cols in zip(y0_halves, halves):
             first_moment(minus_a[:, cols], y, m1_picked[:, cols])
-        for cols in halves:
-            nc.gpsimd.tensor_tensor(minus_step[:, cols], minus_a[:, cols], root[:, cols], ALU.mult)
-        nc.vector.tensor_copy(par_picked[:], par_sb[0][:].indirect(ent_sb[:]))
+        par_picked = work("m2_sb", 0)
+        first, second = halves
+        nc.gpsimd.tensor_tensor(minus_step[:, first], minus_a[:, first], root[:, first], ALU.mult)
+        nc.vector.tensor_copy(par_picked[:, first], par_sb[0][:].indirect(entries(first)))
+        gather(par_picked, par_sb[0], second)
+        nc.vector.tensor_tensor(minus_step[:, second], minus_a[:, second], root[:, second], ALU.mult)
         scatter(0, par_picked, minus_step, whole)
         nc.sync.dma_start(rows(out, 0), par_sb[0][:])
 

@@ -225,23 +225,22 @@ def tile_picked_sadam_none_p_kernel(tc, x_words, x_scales, w1, par, m1, m2, offs
         first_moment(minus_a2[:], ys[2], m1_picked2)
         update(1, par1, step1)
 
-        m2_picked2, root_turned2, step2 = work("square", 1), work("root_turned", 2), work("minus_step", 2)
-        b2 = [
-            turned_sum(number, square2, picked(m2_sb, 2, m2_picked2, cols), cols)
-            for number, cols in zip((5, 6), halves)
-        ]
-        square3 = square_of(3, work("m2_sb", 2))
-        root2 = [root_of(b, root_turned2, number, cols) for b, number, cols in zip(b2, (7, 4), halves)]
-        after_root2 = keep.tile([P, 3, S], F32, name="square1")
-        m1_picked3 = picked(m1_sb, 3, after_root2[:, 1, :], whole)
+        root_turned2, step2 = work("root_turned", 2), work("minus_step", 2)
+        m2_picked2 = picked(m2_sb, 2, work("square", 1), whole)
+        b2 = turned_sum(5, square2, m2_picked2, whole)
+        m1_picked3 = picked(m1_sb, 3, work("m1_picked", 3), whole)
+        root2 = [root_of(b2, root_turned2, number, cols) for number, cols in zip((7, 4), halves)]
+        after_root2 = keep.tile([P, 2, S], F32, name="square1")
         par2 = picked(par_sb, 2, after_root2[:, 0, :], whole)
         for root, cols in zip(root2, halves):
             product(step2, root, minus_a2, cols)
-        minus_a3 = work("root_turned", 2)
-        first_moment(minus_a3[:], ys[3], m1_picked3)
+        terms3 = keep.tile([P, 2, S], F32, name="root_turned2")
+        square3, minus_a3 = terms3[:, 0, :], terms3[:, 1, :]
+        nc.scalar.activation(square3, project(3, 2, whole), ACT.Square, scale=SQUARE_SCALE)
+        first_moment(minus_a3, ys[3], m1_picked3[:])
         update(2, par2, step2)
 
-        m2_picked3 = after_root2[:, 2, :]
+        m2_picked3 = after_root2[:, 1, :]
         root_turned3, step3 = (work(name, 3) for name in ("root_turned", "minus_step"))
         b3 = [
             turned_sum(number, square3, picked(m2_sb, 3, m2_picked3, cols), cols)

import math
from contextlib import ExitStack

import concourse.mybir as mybir
from concourse.masks import make_identity

K, T, S, N, U = 512, 2048, 512, 512, 1024
FLOPS = 2 * K * N * S

F32 = mybir.dt.float32
BF16 = mybir.dt.bfloat16
I32 = mybir.dt.int32
U32 = mybir.dt.uint32
U16 = mybir.dt.uint16
U8 = mybir.dt.uint8
FP8X4 = mybir.dt.float8_e4m3fn_x4
ACT = mybir.ActivationFunctionType
ALU = mybir.AluOpType

P = 128
PACK = 4
GROUP = 16
QUADRANT = 32
BANKS = 8
TILES = N // P
BLOCKS = S // P
SCALE_ROWS = K // 32
ROWS_PER_QUADRANT = SCALE_ROWS * QUADRANT // P
SCALE_FIRST = P - SCALE_ROWS
VECTOR_SHARE = 96
W_FIRST = 256
SQUARE_SCALE = 1.0 / math.sqrt(7.0)
ROOT_SCALE = 0.875 / 0.375**2


def tile_picked_sadam_none_p_kernel(tc, x_words, x_scales, w1, par, m1, m2, offs, ent, out):
    nc = tc.nc
    with ExitStack() as ctx:
        lists = ctx.enter_context(tc.tile_pool(name="lists", bufs=1))
        keep = ctx.enter_context(tc.tile_pool(name="keep", bufs=1))
        psum = ctx.enter_context(tc.psum_pool(name="psum", bufs=1))

        offs_sb = lists.tile([P, S // GROUP], U16, name="offs_sb")
        ent_sb = lists.tile([P, S // GROUP], U16, name="ent_sb")

        def rows(table, t):
            return table.rearrange("(p t) u -> t p u", t=TILES)[t]

        x_plane = keep.tile([P, S], U8, name="x_plane", align_bytes=64)
        nc.gpsimd.memset(x_plane[:].bitcast(I32), 0)
        scale_table = keep.tile([P, T], U8, name="scale_table", align_bytes=64)
        nc.gpsimd.memset(scale_table[:SCALE_FIRST, :].bitcast(I32), 0)
        seven = keep.tile([P, 1], F32, name="seven")
        nc.vector.memset(seven[:], 7.0)
        first_scale = keep.tile([P, 1], F32, name="first_scale")
        nc.scalar.activation(first_scale[:], seven[:], ACT.Abs_reciprocal_sqrt)

        w_raw = keep.tile([P, PACK, N], F32, name="w_raw")
        w_rows = w1.rearrange("(p j) n -> p (j n)", j=PACK)
        w_flat = w_raw[:].rearrange("p j n -> p (j n)")
        nc.sync.dma_start(w_flat[:, :W_FIRST], w_rows[:, :W_FIRST])
        nc.sync.dma_start(offs_sb[:], offs)
        nc.sync.dma_start(scale_table[SCALE_FIRST:, :].bitcast(I32), x_scales[0].bitcast(I32))
        nc.sync.dma_start(w_flat[:, W_FIRST:], w_rows[:, W_FIRST:])
        word_table = keep.tile([P, T], I32, name="word_table", align_bytes=64)
        nc.sync.dma_start(word_table[:], x_words[0].rearrange("p c r -> p (c r)").bitcast(I32))
        nc.sync.dma_start(ent_sb[:], ent)

        ident = keep.tile([P, P], F32, name="ident")
        make_identity(nc, ident[:])

        x_codes = keep.tile([P, S], U32, name="x_codes", align_bytes=64)
        scale_picked = keep.tile([P, S], U8, name="scale_picked", align_bytes=64)
        nc.vector.tensor_copy(scale_picked[:], scale_table[:].indirect(offs_sb[:]))
        for quadrant in range(P // QUADRANT):
            source = SCALE_FIRST + ROWS_PER_QUADRANT * quadrant
            target = QUADRANT * quadrant
            queue = nc.scalar if quadrant % 2 else nc.sync
            queue.dma_start(
                x_plane[target : target + ROWS_PER_QUADRANT, :].bitcast(I32),
                scale_picked[source : source + ROWS_PER_QUADRANT, :].bitcast(I32),
            )
        halves = [slice(h * S // 2, (h + 1) * S // 2) for h in range(2)]
        for cols in halves:
            picks = offs_sb[:, cols.start // GROUP : cols.stop // GROUP]
            nc.vector.tensor_copy(x_codes[:, cols], word_table[:].bitcast(U32).indirect(picks))

        m2_sb = [keep.tile([P, U], F32, name="m2_sb%d" % t) for t in range(TILES)]
        m1_sb = [keep.tile([P, U], F32, name="m1_sb%d" % t) for t in range(TILES)]
        par_sb = [keep.tile([P, U], F32, name="par_sb%d" % t) for t in range(TILES)]
        tables = {"m2": (m2_sb, m2), "m1": (m1_sb, m1), "par": (par_sb, par)}
        for name, t in (
            ("m1", 0), ("m2", 0), ("par", 0),
            ("m2", 1), ("m1", 1), ("m1", 2), ("par", 1),
            ("m2", 2), ("m1", 3), ("par", 2),
            ("m2", 3), ("par", 3),
        ):
            tiles, table = tables[name]
            nc.sync.dma_start(tiles[t][:], rows(table, t))

        w_grouped = keep.tile([P, N * PACK], BF16, name="w_grouped", align_bytes=64)
        grouped_view = w_grouped[:].rearrange("p (t m j) -> p m t j", t=TILES, j=PACK)
        raw_view = w_raw[:].rearrange("p j (m t) -> p m t j", t=TILES)
        nc.vector.tensor_copy(grouped_view[:, :VECTOR_SHARE], raw_view[:, :VECTOR_SHARE])
        nc.scalar.copy(grouped_view[:, VECTOR_SHARE:], raw_view[:, VECTOR_SHARE:])
        w_codes = keep.tile([P, N], U32, name="w_codes", align_bytes=64)
        w_plane = keep.tile([P, N], U8, name="w_plane", align_bytes=64)
        nc.vector.quantize_mx(out=w_codes[:].bitcast(FP8X4), scales=w_plane[:], in_=w_grouped[:])

        def bank(number):
            return psum.tile([P, S], F32, name="bank%d" % number)

        def turn(target, source, start, stop, part):
            blocks = range(part.start // P, part.stop // P)
            for c in blocks:
                cols = slice(c * P, (c + 1) * P)
                nc.tensor.matmul(
                    target[:, cols],
                    source[:, cols],
                    ident[:],
                    start=start and c == blocks[0],
                    stop=stop and c == blocks[-1],
                    is_transpose=True,
                )

        def project(t, number, picks):
            cols = slice(t * P, (t + 1) * P)
            y = bank(number)[:, : picks.stop - picks.start]
            nc.tensor.matmul_mx(
                out=y,
                lhsT=w_codes[:, cols].bitcast(FP8X4),
                lhsT_scale=w_plane[:, cols],
                rhs=x_codes[:, picks].bitcast(FP8X4),
                rhs_scale=x_plane[:, picks],
                start=True,
                stop=True,
            )
            return y

        def entries(cols):
            return ent_sb[:, cols.start // GROUP : cols.stop // GROUP]

        def gather(picked, window, cols):
            nc.scalar.activation(picked[:, cols], window[:].indirect(entries(cols)), ACT.Copy)

        def scatter(t, par_picked, minus_step, cols):
            nc.vector.tensor_tensor(
                par_sb[t][:].indirect(entries(cols)), par_picked[:, cols], minus_step[:, cols], ALU.add
            )

        def work(name, t):
            return keep.tile([P, S], F32, name="%s%d" % (name, t))

        whole = slice(0, S)
        y0_halves = [project(0, number, cols) for number, cols in zip((0, BANKS - 1), halves)]
        ys = [None] + [project(t, t, whole) for t in range(1, TILES)]

        def first_moment(minus_a, y, m1_picked):
            nc.vector.scalar_tensor_tensor(minus_a, y, -1.0 / 3.0, m1_picked, ALU.mult, ALU.subtract)

        m1_picked, b_sum, root, minus_step = (
            work(name, 0) for name in ("m1_picked", "b_sum", "root", "minus_step")
        )
        nc.vector.tensor_copy(m1_picked[:], m1_sb[0][:].indirect(ent_sb[:]))
        for h, (y, cols) in enumerate(zip(y0_halves, halves)):
            square = keep.tile([P, S // 2], F32, name="square_half%d" % h)
            nc.scalar.activation(square[:], y, ACT.Square, scale=SQUARE_SCALE if h else first_scale[:])
            nc.vector.tensor_tensor(b_sum[:, cols], m2_sb[0][:].indirect(entries(cols)), square[:], ALU.add)
            nc.scalar.activation(root[:, cols], b_sum[:, cols], ACT.Abs_reciprocal_sqrt, scale=ROOT_SCALE)
        minus_a = keep.tile([P, S], F32, name="square_half0")
        for y, cols in zip(y0_halves, halves):
            first_moment(minus_a[:, cols], y, m1_picked[:, cols])
        par_picked = work("m2_sb", 0)
        first, second = halves
        nc.gpsimd.tensor_tensor(minus_step[:, first], minus_a[:, first], root[:, first], ALU.mult)
        nc.vector.tensor_copy(par_picked[:, first], par_sb[0][:].indirect(entries(first)))
        gather(par_picked, par_sb[0], second)
        nc.vector.tensor_tensor(minus_step[:, second], minus_a[:, second], root[:, second], ALU.mult)
        scatter(0, par_picked, minus_step, whole)
        nc.sync.dma_start(rows(out, 0), par_sb[0][:])

        def picked(table, t, tile, cols):
            gather(tile, table[t], cols)
            return tile

        def square_of(t, tile):
            nc.scalar.activation(tile[:], ys[t], ACT.Square, scale=SQUARE_SCALE)
            return tile

        def turned_sum(number, square, m2_picked, cols):
            b_turned = bank(number)
            turn(b_turned, square, True, False, cols)
            turn(b_turned, m2_picked, False, True, cols)
            return b_turned

        def root_of(b_turned, root_turned, number, cols):
            nc.scalar.activation(
                root_turned[:, cols], b_turned[:, cols], ACT.Abs_reciprocal_sqrt, scale=ROOT_SCALE
            )
            root = bank(number)
            turn(root, root_turned, True, True, cols)
            return root

        def product(minus_step, root, minus_a, cols):
            nc.vector.tensor_tensor(minus_step[:, cols], root[:, cols], minus_a[:, cols], ALU.mult)

        def update(t, par_picked, minus_step):
            scatter(t, par_picked, minus_step, whole)
            nc.sync.dma_start(rows(out, t), par_sb[t][:])

        square1 = square_of(1, work("square", 1))
        square2 = square_of(2, work("square", 2))
        b1 = turned_sum(4, square1, picked(m2_sb, 1, work("m2_picked", 1), whole), whole)
        m1_picked1 = picked(m1_sb, 1, work("m1_picked", 1), whole)
        root1 = root_of(b1, work("root_turned", 1), 0, whole)
        after_root1 = keep.tile([P, 2, S], F32, name="m2_picked1")
        m1_picked2 = picked(m1_sb, 2, after_root1[:, 0, :], whole)
        par1 = picked(par_sb, 1, after_root1[:, 1, :], whole)
        minus_a1, step1 = work("minus_a", 1), work("minus_step", 1)
        for cols in halves:
            first_moment(minus_a1[:, cols], ys[1][:, cols], m1_picked1[:, cols])
        for cols in halves:
            product(step1, root1, minus_a1, cols)
        minus_a2 = work("root_turned", 1)
        first_moment(minus_a2[:], ys[2], m1_picked2)
        update(1, par1, step1)

        root_turned2, step2 = work("root_turned", 2), work("minus_step", 2)
        m2_picked2 = picked(m2_sb, 2, work("square", 1), whole)
        b2 = turned_sum(5, square2, m2_picked2, whole)
        m1_picked3 = picked(m1_sb, 3, work("m1_picked", 3), whole)
        root2 = [root_of(b2, root_turned2, number, cols) for number, cols in zip((7, 4), halves)]
        after_root2 = keep.tile([P, 2, S], F32, name="square1")
        par2 = picked(par_sb, 2, after_root2[:, 0, :], whole)
        for root, cols in zip(root2, halves):
            product(step2, root, minus_a2, cols)
        terms3 = keep.tile([P, 2, S], F32, name="root_turned2")
        square3, minus_a3 = terms3[:, 0, :], terms3[:, 1, :]
        nc.scalar.activation(square3, project(3, 2, whole), ACT.Square, scale=SQUARE_SCALE)
        first_moment(minus_a3, ys[3], m1_picked3[:])
        update(2, par2, step2)

        m2_picked3 = after_root2[:, 1, :]
        root_turned3, step3 = (work(name, 3) for name in ("root_turned", "minus_step"))
        b3 = [
            turned_sum(number, square3, picked(m2_sb, 3, m2_picked3, cols), cols)
            for number, cols in zip((0, 5), halves)
        ]
        par3 = picked(par_sb, 3, work("par_picked", 3), halves[0])
        root3 = [root_of(b, root_turned3, number, cols) for b, number, cols in zip(b3, (6, 1), halves)]
        picked(par_sb, 3, par3, halves[1])
        for root, cols in zip(root3, halves):
            product(step3, root, minus_a3, cols)
        update(3, par3, step3)
